import numpy as np
import ml_dtypes


def mxq(x, axis, fmt="e4m3"):
    dtype, down = {"e4m3": (ml_dtypes.float8_e4m3fn, 7), "e5m2": (ml_dtypes.float8_e5m2, 14)}[fmt]
    v = np.moveaxis(np.asarray(x, np.float32).astype(ml_dtypes.bfloat16).astype(np.float64), axis, -1)
    blocks = v.reshape(v.shape[:-1] + (-1, 32))
    amax = np.abs(blocks).max(-1, keepdims=True)
    byte = np.maximum(np.where(amax > 0, np.frexp(amax)[1] - 1 + 127, 0) - down, 1)
    scale = np.exp2(byte - 127.0)
    codes = (blocks / scale).astype(np.float32).astype(dtype).astype(np.float64)
    return np.moveaxis((codes * scale).reshape(v.shape), -1, axis)


WIDE = False


def mx_kscale(k):
    if not WIDE:
        return np.ones(k)
    levels = np.array([10, -10, 5, -5, 0])
    if k % 512:
        return np.exp2(np.random.permutation(np.resize(levels, k // 32))).repeat(32)
    a = np.empty((k // 512, 16))
    for p in range(k // 512):
        a[p, :8] = np.random.permutation(np.resize(levels, 8))
        for g in range(8):
            far = levels[np.abs(levels - a[p, g]) >= 10]
            a[p, g + 8] = far[np.random.randint(len(far))]
    return np.exp2(a.ravel()).repeat(32)


def f64(x):
    return np.asarray(x).astype(np.float64)


def striped(idx):
    return np.tile(idx.reshape(-1, 16).T, (8, 1)).astype(np.uint16)


def unstriped(offs):
    return offs[:16].T.reshape(-1).astype(np.int64)


def pack_weight(w):
    k, n = w.shape
    w = f64(np.asarray(w, np.float32).astype(ml_dtypes.bfloat16)).reshape(k // 32, 32, n)
    amax = np.abs(w).max(1)
    byte = np.clip(np.where(amax > 0, np.frexp(amax)[1] - 1 + 127 - 7, 1), 1, 254)
    scaled = (w * np.exp2(127.0 - byte)[:, None, :]).reshape(k, n).astype(np.float32)
    words = np.ascontiguousarray(scaled.reshape(k // 512, 128, 4, n).transpose(0, 1, 3, 2)).astype(ml_dtypes.float8_e4m3fn).view(np.uint8)
    return words, np.ascontiguousarray(byte.astype(np.uint8).reshape(k // 512, 16, n))


def unpack_weight(words, scales):
    g, p, n, _ = words.shape
    vals = np.ascontiguousarray(words).view(ml_dtypes.float8_e4m3fn).astype(np.float64) * np.repeat(np.exp2(scales.astype(np.float64) - 127.0), 8, axis=1)[..., None]
    return vals.transpose(0, 1, 3, 2).reshape(g * 512, n)


def silu(v):
    return v / (1.0 + np.exp(-np.maximum(v, -700.0)))


K, T, E, C, N = 512, 4096, 8, 256, 128


def by_expert(wq, xq):
    return np.concatenate([wq[e].T @ xq[:, e * C:(e + 1) * C] for e in range(E)], axis=1)


def setup_inputs():
    n = np.random.standard_normal
    s = mx_kscale(K)[:, None]
    packed = [pack_weight(m) for m in n((E, K, N)) / np.sqrt(K) / s[None]]
    return {
        "xT": (n((K, T)) * s).astype(np.float32),
        "xr": n((N, T)).astype(np.float32),
        "w_words": np.stack([m[0] for m in packed]),
        "w_scales": np.stack([m[1] for m in packed]),
        "b": (0.3 * n((N, E))).astype(np.float32),
        "gate": np.tile(np.random.uniform(0.2, 1.0, E * C), (N, 1)).astype(np.float32),
        "offs": striped(np.random.permutation(T)[:E * C]),
    }


def reference(xT, xr, w_words, w_scales, b, gate, offs):
    idx = unstriped(offs)
    w = np.stack([unpack_weight(w_words[e], w_scales[e]) for e in range(E)])
    xq = mxq(f64(xT)[:, idx], 0, "e4m3")
    y = by_expert(w, xq)
    y = silu(y + np.repeat(f64(b), C, axis=1))
    out = f64(xr).copy()
    out[:, idx] += f64(gate) * y
    return out

@@ -1,0 +1,140 @@
+from contextlib import ExitStack
+
+import concourse.mybir as mybir
+
+K, T, E, C, N = 512, 4096, 8, 256, 128
+SLOTS = E * C
+FLOPS = 2 * SLOTS * K * N
+
+F32 = mybir.dt.float32
+BF16 = mybir.dt.bfloat16
+U32 = mybir.dt.uint32
+I32 = mybir.dt.int32
+U16 = mybir.dt.uint16
+U8 = mybir.dt.uint8
+FP8X4 = mybir.dt.float8_e4m3fn_x4
+MULT = mybir.AluOpType.mult
+ADD = mybir.AluOpType.add
+SILU = mybir.ActivationFunctionType.Silu
+
+P = 128
+PACK = 4
+CHUNK = 512
+CHUNKS = SLOTS // CHUNK
+PER_CHUNK = CHUNK // C
+
+
+def tile_moe_res_lin_silu_kernel(tc, xT, xr, w_words, w_scales, b, gate, offs, out):
+    nc = tc.nc
+    with ExitStack() as ctx:
+        keep = ctx.enter_context(tc.tile_pool(name="keep", bufs=1))
+        psum = ctx.enter_context(tc.psum_pool(name="psum", bufs=1))
+
+        offsets = keep.tile([P, SLOTS // 16], U16, name="offsets")
+        planes = [keep.tile([P, T], F32, name=f"plane{t}") for t in range(PACK)]
+        w_codes = keep.tile([P, E, N], U32, name="w_codes", align_bytes=64)
+        w_bytes = keep.tile([P, E, N], U8, name="w_bytes", align_bytes=64)
+        bias = keep.tile([P, E], F32, name="bias")
+        weight = keep.tile([P, SLOTS], F32, name="weight")
+        early = keep.tile([P, 2, SLOTS], F32, name="early", align_bytes=64)
+        shared = keep.tile([P, 3, CHUNK], F32, name="shared", align_bytes=64)
+        own = keep.tile([P, 2, 2 * CHUNK], F32, name="own", align_bytes=64)
+        grouped = keep.tile([P, SLOTS, PACK], BF16, name="grouped", align_bytes=64)
+        y = keep.tile([P, SLOTS], F32, name="y")
+        window = keep.tile([P, T], F32, name="window")
+        warm = keep.tile([P, 1], F32, name="warm")
+
+        nc.vector.memset(w_bytes[:].bitcast(I32), 0)
+        nc.sync.dma_start(offsets[:], offs)
+        x_rows = xT.rearrange("(p t) w -> p t w", t=PACK)
+        for t in range(PACK):
+            nc.sync.dma_start(planes[t][:], x_rows[:, t, :])
+        nc.sync.dma_start(w_codes[:].bitcast(I32), w_words.rearrange("e a p n r -> p (e a) (n r)").bitcast(I32))
+        nc.sync.dma_start(weight[:], gate)
+
+        nc.vector.memset(warm[:], 0.0)
+        s_rows = w_scales.rearrange("e a q n -> q (e a) n")
+        for q in range(4):
+            nc.scalar.dma_start(w_bytes[32 * q : 32 * q + 4, :, :].bitcast(I32), s_rows[4 * q : 4 * q + 4, :, :].bitcast(I32))
+        nc.scalar.dma_start(bias[:], b)
+        nc.gpsimd.memset(window[:], 0.0)
+        nc.scalar.activation(warm[:], warm[:], SILU)
+
+        residual = keep.tile([P, T], F32, name="residual")
+        for i in range(4):
+            nc.sync.dma_start(residual[:, i * (T // 4) : (i + 1) * (T // 4)], xr[:, i * (T // 4) : (i + 1) * (T // 4)])
+
+        late = [shared[:, 1:3, :], own[:, :, 0:CHUNK], own[:, :, CHUNK : 2 * CHUNK], shared[:, 0:3:2, :]]
+
+        def gather(t, first, last, into):
+            nc.vector.tensor_copy(into, planes[t][:].indirect(offsets[:, first // 16 : last // 16]))
+
+        def late_gather(t, c):
+            gather(t, c * CHUNK, (c + 1) * CHUNK, late[c][:, t - 2, :])
+
+        def interleave(t, first, last, pair):
+            nc.scalar.copy(grouped[:, first:last, t : t + 2], pair.rearrange("p t n -> p n t"))
+
+        def late_interleave(c):
+            interleave(2, c * CHUNK, (c + 1) * CHUNK, late[c])
+
+        banks = [psum.tile([P, C], F32, name=f"bank{e}") for e in range(E)]
+
+        def multiply(first, last):
+            codes = keep.tile([P, last - first], U32, name=f"codes{first}", align_bytes=64)
+            scales = keep.tile([P, last - first], U8, name=f"scales{first}", align_bytes=64)
+            nc.vector.quantize_mx(
+                out=codes[:].bitcast(FP8X4),
+                scales=scales[:],
+                in_=grouped[:, first:last, :].rearrange("p n t -> p (n t)"),
+            )
+            for e in range(first // C, last // C):
+                cols = slice(e * C - first, e * C - first + C)
+                nc.tensor.matmul_mx(
+                    out=banks[e][:],
+                    lhsT=w_codes[:, e, :].bitcast(FP8X4),
+                    lhsT_scale=w_bytes[:, e, :],
+                    rhs=codes[:, cols].bitcast(FP8X4),
+                    rhs_scale=scales[:, cols],
+                    start=True,
+                    stop=True,
+                )
+                nc.scalar.activation(y[:, e * C : (e + 1) * C], banks[e][:], SILU, bias=bias[:, e : e + 1])
+
+        def scatter(first, last):
+            nc.vector.tensor_tensor(
+                window[:].indirect(offsets[:, first // 16 : last // 16]), y[:, first:last], weight[:, first:last], MULT
+            )
+
+        gather(0, 0, SLOTS, early[:, 0, :])
+        for h in range(2):
+            half = slice(h * 1024, h * 1024 + 1024)
+            gather(1, half.start, half.stop, early[:, 1, half])
+            interleave(0, half.start, half.stop, early[:, :, half])
+        late_gather(2, 0)
+        gather(2, CHUNK, 3 * CHUNK, own[:, 0, :])
+        late_gather(2, 3)
+        late_gather(3, 0)
+        late_interleave(0)
+        late_gather(3, 1)
+        late_interleave(1)
+        late_gather(3, 2)
+        multiply(0, 512)
+        late_gather(3, 3)
+        multiply(512, 1024)
+        late_interleave(2)
+        scatter(0, 512)
+        multiply(1024, 1536)
+        late_interleave(3)
+        scatter(512, 1024)
+        multiply(1536, 2048)
+        scatter(1024, 1536)
+        scatter(1536, 2048)
+
+        start = 0
+        for i, width in enumerate((256, 384, 512, 704, 896, 832, 512)):
+            x = residual[:, start : start + width]
+            res = keep.tile([P, width], F32, name=f"res{i}")
+            nc.vector.tensor_tensor(res[:], window[:, start : start + width], x, ADD)
+            nc.sync.dma_start(out[:, start : start + width], res[:])
+            start += width

@@ -15,13 +15,18 @@ U8 = mybir.dt.uint8
 FP8X4 = mybir.dt.float8_e4m3fn_x4
 MULT = mybir.AluOpType.mult
 ADD = mybir.AluOpType.add
+COPY = mybir.ActivationFunctionType.Copy
 SILU = mybir.ActivationFunctionType.Silu
 
 P = 128
 PACK = 4
-CHUNK = 512
-CHUNKS = SLOTS // CHUNK
-PER_CHUNK = CHUNK // C
+CHUNK_EXPERTS = (2, 3, 3)
+LOADS = (
+    ("first", 0, 3072), ("first", 3072, 4096),
+    ("pair", 0, 1536), ("pair", 1536, 3072), ("last", 0, 1024), ("pair", 3072, 3840), ("pair", 3840, 4096),
+    ("last", 1024, 1792), ("last", 1792, 2560), ("last", 2560, 3328), ("last", 3328, 3840), ("last", 3840, 4096),
+)
+STORE_WIDTHS = (256, 384, 512, 704, 896, 832, 512)
 
 
 def tile_moe_res_lin_silu_kernel(tc, xT, xr, w_words, w_scales, b, gate, offs, out):
@@ -30,25 +35,36 @@ def tile_moe_res_lin_silu_kernel(tc, xT, xr, w_words, w_scales, b, gate, offs, o
         keep = ctx.enter_context(tc.tile_pool(name="keep", bufs=1))
         psum = ctx.enter_context(tc.psum_pool(name="psum", bufs=1))
 
+        firsts = [sum(CHUNK_EXPERTS[:c]) for c in range(len(CHUNK_EXPERTS))]
+        chunks = [range(f, f + n) for f, n in zip(firsts, CHUNK_EXPERTS)]
+
         offsets = keep.tile([P, SLOTS // 16], U16, name="offsets")
-        planes = [keep.tile([P, T], F32, name=f"plane{t}") for t in range(PACK)]
+        pairs = keep.tile([P, T, 2], BF16, name="pairs", align_bytes=64)
+        first_plane = keep.tile([P, T], BF16, name="first_plane", align_bytes=64)
+        last_plane = keep.tile([P, T], BF16, name="last_plane", align_bytes=64)
         w_codes = keep.tile([P, E, N], U32, name="w_codes", align_bytes=64)
         w_bytes = keep.tile([P, E, N], U8, name="w_bytes", align_bytes=64)
         bias = keep.tile([P, E], F32, name="bias")
         weight = keep.tile([P, SLOTS], F32, name="weight")
-        early = keep.tile([P, 2, SLOTS], F32, name="early", align_bytes=64)
-        shared = keep.tile([P, 3, CHUNK], F32, name="shared", align_bytes=64)
-        own = keep.tile([P, 2, 2 * CHUNK], F32, name="own", align_bytes=64)
-        grouped = keep.tile([P, SLOTS, PACK], BF16, name="grouped", align_bytes=64)
-        y = keep.tile([P, SLOTS], F32, name="y")
+        widths = [len(ex) * C for ex in chunks]
+        shared = keep.tile([P, T], BF16, name="shared", align_bytes=64)
+        grouped = [shared[:, : PACK * widths[0]]]
+        grouped.extend(keep.tile([P, PACK * widths[c]], BF16, name=f"grouped{c}", align_bytes=64)[:] for c in (1, 2))
+        y = [keep.tile([P, len(ex) * C], F32, name=f"y{c}") for c, ex in enumerate(chunks)]
         window = keep.tile([P, T], F32, name="window")
+        residual = keep.tile([P, T], F32, name="residual")
         warm = keep.tile([P, 1], F32, name="warm")
+        banks = [psum.tile([P, C], F32, name=f"bank{e}") for e in range(E)]
 
         nc.vector.memset(w_bytes[:].bitcast(I32), 0)
         nc.sync.dma_start(offsets[:], offs)
         x_rows = xT.rearrange("(p t) w -> p t w", t=PACK)
-        for t in range(PACK):
-            nc.sync.dma_start(planes[t][:], x_rows[:, t, :])
+        rows = {"pair": slice(0, 2), "first": slice(2, 3), "last": slice(3, 4)}
+        raw = {}
+        for kind, first, last in LOADS:
+            count = rows[kind].stop - rows[kind].start
+            raw[kind, first] = keep.tile([P, count, last - first], F32, name=f"raw{kind}{first}")
+            nc.sync.dma_start(raw[kind, first][:], x_rows[:, rows[kind], first:last])
         nc.sync.dma_start(w_codes[:].bitcast(I32), w_words.rearrange("e a p n r -> p (e a) (n r)").bitcast(I32))
         nc.sync.dma_start(weight[:], gate)
 
@@ -60,36 +76,43 @@ def tile_moe_res_lin_silu_kernel(tc, xT, xr, w_words, w_scales, b, gate, offs, o
         nc.gpsimd.memset(window[:], 0.0)
         nc.scalar.activation(warm[:], warm[:], SILU)
 
-        residual = keep.tile([P, T], F32, name="residual")
         for i in range(4):
             nc.sync.dma_start(residual[:, i * (T // 4) : (i + 1) * (T // 4)], xr[:, i * (T // 4) : (i + 1) * (T // 4)])
 
-        late = [shared[:, 1:3, :], own[:, :, 0:CHUNK], own[:, :, CHUNK : 2 * CHUNK], shared[:, 0:3:2, :]]
+        def listed(c):
+            return offsets[:, chunks[c].start * C // 16 : chunks[c].stop * C // 16]
 
-        def gather(t, first, last, into):
-            nc.vector.tensor_copy(into, planes[t][:].indirect(offsets[:, first // 16 : last // 16]))
+        def cast(kind, first, last):
+            src = raw[kind, first]
+            if kind == "pair":
+                nc.vector.tensor_copy(pairs[:, first:last, :], src[:].rearrange("p t n -> p n t"))
+            elif kind == "first":
+                nc.vector.tensor_copy(first_plane[:, first:last], src[:, 0, :])
+            else:
+                nc.scalar.copy(last_plane[:, first:last], src[:, 0, :])
 
-        def late_gather(t, c):
-            gather(t, c * CHUNK, (c + 1) * CHUNK, late[c][:, t - 2, :])
+        def gather_pair(c):
+            words = pairs[:].rearrange("p n t -> p (n t)").bitcast(U32)
+            into = grouped[c].bitcast(U32).rearrange("p (n u) -> p n u", u=2)[:, :, 0]
+            nc.vector.tensor_copy(into, words.indirect(listed(c)))
 
-        def interleave(t, first, last, pair):
-            nc.scalar.copy(grouped[:, first:last, t : t + 2], pair.rearrange("p t n -> p n t"))
+        def gather_plane(plane, t, c):
+            into = grouped[c].rearrange("p (n t) -> p n t", t=PACK)[:, :, t]
+            nc.scalar.activation(into, plane[:].indirect(listed(c)), COPY)
 
-        def late_interleave(c):
-            interleave(2, c * CHUNK, (c + 1) * CHUNK, late[c])
-
-        banks = [psum.tile([P, C], F32, name=f"bank{e}") for e in range(E)]
-
-        def multiply(first, last):
-            codes = keep.tile([P, last - first], U32, name=f"codes{first}", align_bytes=64)
-            scales = keep.tile([P, last - first], U8, name=f"scales{first}", align_bytes=64)
-            nc.vector.quantize_mx(
-                out=codes[:].bitcast(FP8X4),
-                scales=scales[:],
-                in_=grouped[:, first:last, :].rearrange("p n t -> p (n t)"),
-            )
-            for e in range(first // C, last // C):
-                cols = slice(e * C - first, e * C - first + C)
+        def multiply(c):
+            width = len(chunks[c]) * C
+            codes = keep.tile([P, width], U32, name=f"codes{c}", align_bytes=64)
+            scales = keep.tile([P, width], U8, name=f"scales{c}", align_bytes=64)
+            for first, last in ((0, 2 * C), (2 * C, width)):
+                if last > first:
+                    nc.vector.quantize_mx(
+                        out=codes[:, first:last].bitcast(FP8X4),
+                        scales=scales[:, first:last],
+                        in_=grouped[c][:, PACK * first : PACK * last],
+                    )
+            for i, e in enumerate(chunks[c]):
+                cols = slice(i * C, (i + 1) * C)
                 nc.tensor.matmul_mx(
                     out=banks[e][:],
                     lhsT=w_codes[:, e, :].bitcast(FP8X4),
@@ -99,42 +122,34 @@ def tile_moe_res_lin_silu_kernel(tc, xT, xr, w_words, w_scales, b, gate, offs, o
                     start=True,
                     stop=True,
                 )
-                nc.scalar.activation(y[:, e * C : (e + 1) * C], banks[e][:], SILU, bias=bias[:, e : e + 1])
+                nc.scalar.activation(y[c][:, cols], banks[e][:], SILU, bias=bias[:, e : e + 1])
 
-        def scatter(first, last):
-            nc.vector.tensor_tensor(
-                window[:].indirect(offsets[:, first // 16 : last // 16]), y[:, first:last], weight[:, first:last], MULT
-            )
+        def scatter(c):
+            slots = slice(chunks[c].start * C, chunks[c].stop * C)
+            nc.vector.tensor_tensor(window[:].indirect(listed(c)), y[c][:], weight[:, slots], MULT)
 
-        gather(0, 0, SLOTS, early[:, 0, :])
-        for h in range(2):
-            half = slice(h * 1024, h * 1024 + 1024)
-            gather(1, half.start, half.stop, early[:, 1, half])
-            interleave(0, half.start, half.stop, early[:, :, half])
-        late_gather(2, 0)
-        gather(2, CHUNK, 3 * CHUNK, own[:, 0, :])
-        late_gather(2, 3)
-        late_gather(3, 0)
-        late_interleave(0)
-        late_gather(3, 1)
-        late_interleave(1)
-        late_gather(3, 2)
-        multiply(0, 512)
-        late_gather(3, 3)
-        multiply(512, 1024)
-        late_interleave(2)
-        scatter(0, 512)
-        multiply(1024, 1536)
-        late_interleave(3)
-        scatter(512, 1024)
-        multiply(1536, 2048)
-        scatter(1024, 1536)
-        scatter(1536, 2048)
+        for load in LOADS[:2]:
+            cast(*load)
+        for c in range(len(chunks)):
+            gather_plane(first_plane, 2, c)
+        for load in LOADS[2:]:
+            cast(*load)
+        for c in range(len(chunks)):
+            gather_pair(c)
+        gather_plane(last_plane, 3, 0)
+        gather_plane(last_plane, 3, 1)
+        multiply(0)
+        nc.vector.tensor_copy(shared[:], last_plane[:])
+        gather_plane(shared, 3, 2)
+        multiply(1)
+        scatter(0)
+        multiply(2)
+        scatter(1)
+        scatter(2)
 
         start = 0
-        for i, width in enumerate((256, 384, 512, 704, 896, 832, 512)):
-            x = residual[:, start : start + width]
+        for i, width in enumerate(STORE_WIDTHS):
             res = keep.tile([P, width], F32, name=f"res{i}")
-            nc.vector.tensor_tensor(res[:], window[:, start : start + width], x, ADD)
+            nc.vector.tensor_tensor(res[:], window[:, start : start + width], residual[:, start : start + width], ADD)
             nc.sync.dma_start(out[:, start : start + width], res[:])
             start += width

@@ -20,11 +20,11 @@ SILU = mybir.ActivationFunctionType.Silu
 
 P = 128
 PACK = 4
-CHUNK_EXPERTS = (2, 3, 3)
+CHUNK_EXPERTS = (2, 2, 4)
 LOADS = (
     ("first", 0, 3072), ("first", 3072, 4096),
-    ("pair", 0, 1536), ("pair", 1536, 3072), ("last", 0, 1024), ("pair", 3072, 3840), ("pair", 3840, 4096),
-    ("last", 1024, 1792), ("last", 1792, 2560), ("last", 2560, 3328), ("last", 3328, 3840), ("last", 3840, 4096),
+    ("pair", 0, 1536), ("pair", 1536, 3072), ("pair", 3072, 3840), ("pair", 3840, 4096),
+    ("last", 0, 640), ("last", 640, 1344), ("last", 1344, 2048), ("last", 2048, 2752), ("last", 2752, 3456), ("last", 3456, 4096),
 )
 STORE_WIDTHS = (256, 384, 512, 704, 896, 832, 512)
 
@@ -42,17 +42,15 @@ def tile_moe_res_lin_silu_kernel(tc, xT, xr, w_words, w_scales, b, gate, offs, o
         pairs = keep.tile([P, T, 2], BF16, name="pairs", align_bytes=64)
         first_plane = keep.tile([P, T], BF16, name="first_plane", align_bytes=64)
         last_plane = keep.tile([P, T], BF16, name="last_plane", align_bytes=64)
-        w_codes = keep.tile([P, E, N], U32, name="w_codes", align_bytes=64)
+        w_codes = [keep.tile([P, E // 2, N], U32, name=f"w_codes{h}", align_bytes=64) for h in range(1)]
         w_bytes = keep.tile([P, E, N], U8, name="w_bytes", align_bytes=64)
         bias = keep.tile([P, E], F32, name="bias")
-        weight = keep.tile([P, SLOTS], F32, name="weight")
         widths = [len(ex) * C for ex in chunks]
         shared = keep.tile([P, T], BF16, name="shared", align_bytes=64)
-        grouped = [shared[:, : PACK * widths[0]]]
-        grouped.extend(keep.tile([P, PACK * widths[c]], BF16, name=f"grouped{c}", align_bytes=64)[:] for c in (1, 2))
-        y = [keep.tile([P, len(ex) * C], F32, name=f"y{c}") for c, ex in enumerate(chunks)]
+        grouped = [keep.tile([P, PACK * widths[c]], BF16, name=f"grouped{c}", align_bytes=64)[:] for c in range(len(chunks))]
+        y = [keep.tile([P, widths[c]], F32, name=f"y{c}")[:] for c in (0, 2)]
+        y.insert(1, shared[:, : 2 * widths[1]].bitcast(F32))
         window = keep.tile([P, T], F32, name="window")
-        residual = keep.tile([P, T], F32, name="residual")
         warm = keep.tile([P, 1], F32, name="warm")
         banks = [psum.tile([P, C], F32, name=f"bank{e}") for e in range(E)]
 
@@ -63,21 +61,20 @@ def tile_moe_res_lin_silu_kernel(tc, xT, xr, w_words, w_scales, b, gate, offs, o
         raw = {}
         for kind, first, last in LOADS:
             count = rows[kind].stop - rows[kind].start
-            raw[kind, first] = keep.tile([P, count, last - first], F32, name=f"raw{kind}{first}")
+            raw[kind, first] = keep.tile([P, count, last - first], F32, name=f"raw{kind}{first}", tag=f"raw{kind}{first}")
             nc.sync.dma_start(raw[kind, first][:], x_rows[:, rows[kind], first:last])
-        nc.sync.dma_start(w_codes[:].bitcast(I32), w_words.rearrange("e a p n r -> p (e a) (n r)").bitcast(I32))
-        nc.sync.dma_start(weight[:], gate)
-
-        nc.vector.memset(warm[:], 0.0)
         s_rows = w_scales.rearrange("e a q n -> q (e a) n")
         for q in range(4):
-            nc.scalar.dma_start(w_bytes[32 * q : 32 * q + 4, :, :].bitcast(I32), s_rows[4 * q : 4 * q + 4, :, :].bitcast(I32))
-        nc.scalar.dma_start(bias[:], b)
+            nc.sync.dma_start(w_bytes[32 * q : 32 * q + 4, :, :].bitcast(I32), s_rows[4 * q : 4 * q + 4, :, :].bitcast(I32))
+        w_rows = w_words.rearrange("e a p n r -> p (e a) (n r)").bitcast(I32)
+        nc.sync.dma_start(w_codes[0][:].bitcast(I32), w_rows[:, : E // 2, :])
+        nc.sync.dma_start(bias[:], b)
+        first_weight = keep.tile([P, widths[0]], F32, name="first_weight")
+        nc.sync.dma_start(first_weight[:], gate[:, : widths[0]])
+
+        nc.vector.memset(warm[:], 0.0)
         nc.gpsimd.memset(window[:], 0.0)
         nc.scalar.activation(warm[:], warm[:], SILU)
-
-        for i in range(4):
-            nc.sync.dma_start(residual[:, i * (T // 4) : (i + 1) * (T // 4)], xr[:, i * (T // 4) : (i + 1) * (T // 4)])
 
         def listed(c):
             return offsets[:, chunks[c].start * C // 16 : chunks[c].stop * C // 16]
@@ -104,18 +101,12 @@ def tile_moe_res_lin_silu_kernel(tc, xT, xr, w_words, w_scales, b, gate, offs, o
             width = len(chunks[c]) * C
             codes = keep.tile([P, width], U32, name=f"codes{c}", align_bytes=64)
             scales = keep.tile([P, width], U8, name=f"scales{c}", align_bytes=64)
-            for first, last in ((0, 2 * C), (2 * C, width)):
-                if last > first:
-                    nc.vector.quantize_mx(
-                        out=codes[:, first:last].bitcast(FP8X4),
-                        scales=scales[:, first:last],
-                        in_=grouped[c][:, PACK * first : PACK * last],
-                    )
+            nc.vector.quantize_mx(out=codes[:].bitcast(FP8X4), scales=scales[:], in_=grouped[c])
             for i, e in enumerate(chunks[c]):
                 cols = slice(i * C, (i + 1) * C)
                 nc.tensor.matmul_mx(
                     out=banks[e][:],
-                    lhsT=w_codes[:, e, :].bitcast(FP8X4),
+                    lhsT=w_codes[e // 4][:, e % 4, :].bitcast(FP8X4),
                     lhsT_scale=w_bytes[:, e, :],
                     rhs=codes[:, cols].bitcast(FP8X4),
                     rhs_scale=scales[:, cols],
@@ -125,8 +116,7 @@ def tile_moe_res_lin_silu_kernel(tc, xT, xr, w_words, w_scales, b, gate, offs, o
                 nc.scalar.activation(y[c][:, cols], banks[e][:], SILU, bias=bias[:, e : e + 1])
 
         def scatter(c):
-            slots = slice(chunks[c].start * C, chunks[c].stop * C)
-            nc.vector.tensor_tensor(window[:].indirect(listed(c)), y[c][:], weight[:, slots], MULT)
+            nc.vector.tensor_tensor(window[:].indirect(listed(c)), y[c], weight[c], MULT)
 
         for load in LOADS[:2]:
             cast(*load)
@@ -134,12 +124,20 @@ def tile_moe_res_lin_silu_kernel(tc, xT, xr, w_words, w_scales, b, gate, offs, o
             gather_plane(first_plane, 2, c)
         for load in LOADS[2:]:
             cast(*load)
+        nc.sync.dma_start(shared[:], last_plane[:])
+        w_codes.append(keep.tile([P, E // 2, N], U32, name="w_late", align_bytes=64))
+        nc.sync.dma_start(w_codes[1][:].bitcast(I32), w_rows[:, E // 2 :, :])
+        late = keep.tile([P, SLOTS - widths[0] + T], F32, name="late", tag=f"rawlast{LOADS[-1][1]}")
+        weight = [first_weight[:], late[:, : widths[1]], late[:, widths[1] : SLOTS - widths[0]]]
+        residual = late[:, SLOTS - widths[0] :]
+        nc.sync.dma_start(late[:, : SLOTS - widths[0]], gate[:, widths[0] :])
+        for i in range(2):
+            nc.sync.dma_start(residual[:, i * (T // 2) : (i + 1) * (T // 2)], xr[:, i * (T // 2) : (i + 1) * (T // 2)])
         for c in range(len(chunks)):
             gather_pair(c)
         gather_plane(last_plane, 3, 0)
         gather_plane(last_plane, 3, 1)
         multiply(0)
-        nc.vector.tensor_copy(shared[:], last_plane[:])
         gather_plane(shared, 3, 2)
         multiply(1)
         scatter(0)

@@ -20,11 +20,11 @@ SILU = mybir.ActivationFunctionType.Silu
 
 P = 128
 PACK = 4
-CHUNK_EXPERTS = (2, 2, 4)
+CHUNK_EXPERTS = (2, 2, 2, 2)
 LOADS = (
-    ("first", 0, 3072), ("first", 3072, 4096),
-    ("pair", 0, 1536), ("pair", 1536, 3072), ("pair", 3072, 3840), ("pair", 3840, 4096),
-    ("last", 0, 640), ("last", 640, 1344), ("last", 1344, 2048), ("last", 2048, 2752), ("last", 2752, 3456), ("last", 3456, 4096),
+    ("first", 0, 2048, 0), ("first", 2048, 4096, 640),
+    ("pair", 0, 1536, 0), ("pair", 1536, 2816, 0), ("pair", 2816, 3584, 192), ("pair", 3584, 4096, 160),
+    ("last", 0, 1536, 832), ("last", 1536, 2816, 704), ("last", 2816, 3584, 448), ("last", 3584, 4096, 320),
 )
 STORE_WIDTHS = (256, 384, 512, 704, 896, 832, 512)
 
@@ -46,10 +46,11 @@ def tile_moe_res_lin_silu_kernel(tc, xT, xr, w_words, w_scales, b, gate, offs, o
         w_bytes = keep.tile([P, E, N], U8, name="w_bytes", align_bytes=64)
         bias = keep.tile([P, E], F32, name="bias")
         widths = [len(ex) * C for ex in chunks]
-        shared = keep.tile([P, T], BF16, name="shared", align_bytes=64)
+        again = [keep.tile([P, T], BF16, name=f"again{i}", align_bytes=64) for i in range(2)]
         grouped = [keep.tile([P, PACK * widths[c]], BF16, name=f"grouped{c}", align_bytes=64)[:] for c in range(len(chunks))]
-        y = [keep.tile([P, widths[c]], F32, name=f"y{c}")[:] for c in (0, 2)]
-        y.insert(1, shared[:, : 2 * widths[1]].bitcast(F32))
+        y = [keep.tile([P, widths[0]], F32, name="y0")[:]]
+        y.extend(again[i][:, : 2 * widths[i + 1]].bitcast(F32) for i in range(2))
+        y.append(keep.tile([P, widths[3]], F32, name="y3")[:])
         window = keep.tile([P, T], F32, name="window")
         warm = keep.tile([P, 1], F32, name="warm")
         banks = [psum.tile([P, C], F32, name=f"bank{e}") for e in range(E)]
@@ -59,7 +60,7 @@ def tile_moe_res_lin_silu_kernel(tc, xT, xr, w_words, w_scales, b, gate, offs, o
         x_rows = xT.rearrange("(p t) w -> p t w", t=PACK)
         rows = {"pair": slice(0, 2), "first": slice(2, 3), "last": slice(3, 4)}
         raw = {}
-        for kind, first, last in LOADS:
+        for kind, first, last, share in LOADS:
             count = rows[kind].stop - rows[kind].start
             raw[kind, first] = keep.tile([P, count, last - first], F32, name=f"raw{kind}{first}", tag=f"raw{kind}{first}")
             nc.sync.dma_start(raw[kind, first][:], x_rows[:, rows[kind], first:last])
@@ -79,14 +80,13 @@ def tile_moe_res_lin_silu_kernel(tc, xT, xr, w_words, w_scales, b, gate, offs, o
         def listed(c):
             return offsets[:, chunks[c].start * C // 16 : chunks[c].stop * C // 16]
 
-        def cast(kind, first, last):
-            src = raw[kind, first]
-            if kind == "pair":
-                nc.vector.tensor_copy(pairs[:, first:last, :], src[:].rearrange("p t n -> p n t"))
-            elif kind == "first":
-                nc.vector.tensor_copy(first_plane[:, first:last], src[:, 0, :])
-            else:
-                nc.scalar.copy(last_plane[:, first:last], src[:, 0, :])
+        def cast(kind, first, last, share):
+            src = raw[kind, first][:].rearrange("p t n -> p n t")
+            dst = {"pair": pairs[:], "first": first_plane[:].unsqueeze(2), "last": last_plane[:].unsqueeze(2)}[kind]
+            if share > 0:
+                nc.scalar.copy(dst[:, first : first + share, :], src[:, :share, :])
+            other = nc.gpsimd if kind == "last" else nc.vector
+            other.tensor_copy(dst[:, first + share : last, :], src[:, share:, :])
 
         def gather_pair(c):
             words = pairs[:].rearrange("p n t -> p (n t)").bitcast(U32)
@@ -101,9 +101,16 @@ def tile_moe_res_lin_silu_kernel(tc, xT, xr, w_words, w_scales, b, gate, offs, o
             width = len(chunks[c]) * C
             codes = keep.tile([P, width], U32, name=f"codes{c}", align_bytes=64)
             scales = keep.tile([P, width], U8, name=f"scales{c}", align_bytes=64)
-            nc.vector.quantize_mx(out=codes[:].bitcast(FP8X4), scales=scales[:], in_=grouped[c])
+            if c > 0:
+                nc.vector.quantize_mx(out=codes[:].bitcast(FP8X4), scales=scales[:], in_=grouped[c])
             for i, e in enumerate(chunks[c]):
                 cols = slice(i * C, (i + 1) * C)
+                if c == 0:
+                    nc.vector.quantize_mx(
+                        out=codes[:, cols].bitcast(FP8X4),
+                        scales=scales[:, cols],
+                        in_=grouped[c][:, PACK * cols.start : PACK * cols.stop],
+                    )
                 nc.tensor.matmul_mx(
                     out=banks[e][:],
                     lhsT=w_codes[e // 4][:, e % 4, :].bitcast(FP8X4),
@@ -124,13 +131,14 @@ def tile_moe_res_lin_silu_kernel(tc, xT, xr, w_words, w_scales, b, gate, offs, o
             gather_plane(first_plane, 2, c)
         for load in LOADS[2:]:
             cast(*load)
-        nc.sync.dma_start(shared[:], last_plane[:])
+        nc.sync.dma_start(again[0][:], last_plane[:])
         w_codes.append(keep.tile([P, E // 2, N], U32, name="w_late", align_bytes=64))
         nc.sync.dma_start(w_codes[1][:].bitcast(I32), w_rows[:, E // 2 :, :])
         late = keep.tile([P, SLOTS - widths[0] + T], F32, name="late", tag=f"rawlast{LOADS[-1][1]}")
-        weight = [first_weight[:], late[:, : widths[1]], late[:, widths[1] : SLOTS - widths[0]]]
+        weight = [first_weight[:]] + [late[:, i * widths[1] : (i + 1) * widths[1]] for i in range(3)]
         residual = late[:, SLOTS - widths[0] :]
         nc.sync.dma_start(late[:, : SLOTS - widths[0]], gate[:, widths[0] :])
+        nc.sync.dma_start(again[1][:], last_plane[:])
         for i in range(2):
             nc.sync.dma_start(residual[:, i * (T // 2) : (i + 1) * (T // 2)], xr[:, i * (T // 2) : (i + 1) * (T // 2)])
         for c in range(len(chunks)):
@@ -138,12 +146,15 @@ def tile_moe_res_lin_silu_kernel(tc, xT, xr, w_words, w_scales, b, gate, offs, o
         gather_plane(last_plane, 3, 0)
         gather_plane(last_plane, 3, 1)
         multiply(0)
-        gather_plane(shared, 3, 2)
+        gather_plane(again[0], 3, 2)
         multiply(1)
         scatter(0)
+        gather_plane(again[1], 3, 3)
         multiply(2)
         scatter(1)
+        multiply(3)
         scatter(2)
+        scatter(3)
 
         start = 0
         for i, width in enumerate(STORE_WIDTHS):

@@ -20,12 +20,11 @@ SILU = mybir.ActivationFunctionType.Silu
 
 P = 128
 PACK = 4
-CHUNK_EXPERTS = (2, 2, 2, 2)
-LOADS = (
-    ("first", 0, 2048, 0), ("first", 2048, 4096, 640),
-    ("pair", 0, 1536, 0), ("pair", 1536, 2816, 0), ("pair", 2816, 3584, 192), ("pair", 3584, 4096, 160),
-    ("last", 0, 1536, 832), ("last", 1536, 2816, 704), ("last", 2816, 3584, 448), ("last", 3584, 4096, 320),
-)
+CHUNK = 2 * C
+CHUNKS = SLOTS // CHUNK
+PAIR_PIECES = ((0, 1536, 512), (1536, 2816, 448), (2816, 3584, 256), (3584, 4096, 160))
+THIRD_PIECES = ((0, 1536, 896), (1536, 2816, 768), (2816, 3584, 448), (3584, 4096, 320))
+LAST_PIECES = ((0, 512, 0), (512, 1536, 0), (1536, 2560, 0), (2560, 3584, 640), (3584, 4096, 320))
 STORE_WIDTHS = (256, 384, 512, 704, 896, 832, 512)
 
 
@@ -33,24 +32,22 @@ def tile_moe_res_lin_silu_kernel(tc, xT, xr, w_words, w_scales, b, gate, offs, o
     nc = tc.nc
     with ExitStack() as ctx:
         keep = ctx.enter_context(tc.tile_pool(name="keep", bufs=1))
+        turns = ctx.enter_context(tc.tile_pool(name="turns", bufs=1))
         psum = ctx.enter_context(tc.psum_pool(name="psum", bufs=1))
-
-        firsts = [sum(CHUNK_EXPERTS[:c]) for c in range(len(CHUNK_EXPERTS))]
-        chunks = [range(f, f + n) for f, n in zip(firsts, CHUNK_EXPERTS)]
 
         offsets = keep.tile([P, SLOTS // 16], U16, name="offsets")
         pairs = keep.tile([P, T, 2], BF16, name="pairs", align_bytes=64)
-        first_plane = keep.tile([P, T], BF16, name="first_plane", align_bytes=64)
-        last_plane = keep.tile([P, T], BF16, name="last_plane", align_bytes=64)
-        w_codes = [keep.tile([P, E // 2, N], U32, name=f"w_codes{h}", align_bytes=64) for h in range(1)]
+        third_raw = keep.tile([P, T], F32, name="third_raw")
+        third = keep.tile([P, T], BF16, name="third", align_bytes=64)
+        last_raw = turns.tile([P, T], F32, name="last_raw", offset=8128, align_bytes=64)
+        last = keep.tile([P, T], BF16, name="last", align_bytes=64)
+        last_again = keep.tile([P, T], BF16, name="last_again", align_bytes=64)
+        w_first = keep.tile([P, E // 2, N], U32, name="w_first", align_bytes=64)
         w_bytes = keep.tile([P, E, N], U8, name="w_bytes", align_bytes=64)
         bias = keep.tile([P, E], F32, name="bias")
-        widths = [len(ex) * C for ex in chunks]
-        again = [keep.tile([P, T], BF16, name=f"again{i}", align_bytes=64) for i in range(2)]
-        grouped = [keep.tile([P, PACK * widths[c]], BF16, name=f"grouped{c}", align_bytes=64)[:] for c in range(len(chunks))]
-        y = [keep.tile([P, widths[0]], F32, name="y0")[:]]
-        y.extend(again[i][:, : 2 * widths[i + 1]].bitcast(F32) for i in range(2))
-        y.append(keep.tile([P, widths[3]], F32, name="y3")[:])
+        gate_first = keep.tile([P, CHUNK], F32, name="gate_first")
+        grouped = [keep.tile([P, PACK * CHUNK], BF16, name=f"grouped{c}", align_bytes=64) for c in range(CHUNKS)]
+        y = [keep.tile([P, CHUNK], F32, name=f"y{c}") for c in range(CHUNKS)]
         window = keep.tile([P, T], F32, name="window")
         warm = keep.tile([P, 1], F32, name="warm")
         banks = [psum.tile([P, C], F32, name=f"bank{e}") for e in range(E)]
@@ -58,59 +55,61 @@ def tile_moe_res_lin_silu_kernel(tc, xT, xr, w_words, w_scales, b, gate, offs, o
         nc.vector.memset(w_bytes[:].bitcast(I32), 0)
         nc.sync.dma_start(offsets[:], offs)
         x_rows = xT.rearrange("(p t) w -> p t w", t=PACK)
-        rows = {"pair": slice(0, 2), "first": slice(2, 3), "last": slice(3, 4)}
-        raw = {}
-        for kind, first, last, share in LOADS:
-            count = rows[kind].stop - rows[kind].start
-            raw[kind, first] = keep.tile([P, count, last - first], F32, name=f"raw{kind}{first}", tag=f"raw{kind}{first}")
-            nc.sync.dma_start(raw[kind, first][:], x_rows[:, rows[kind], first:last])
+        pair_raw = []
+        for first, stop, share in PAIR_PIECES:
+            pair_raw.append(keep.tile([P, 2, stop - first], F32, name=f"pair_raw{first}"))
+            nc.sync.dma_start(pair_raw[-1][:], x_rows[:, 0:2, first:stop])
+        for first, stop, share in THIRD_PIECES:
+            nc.sync.dma_start(third_raw[:, first:stop], x_rows[:, 2, first:stop])
+        for first, stop, share in LAST_PIECES:
+            nc.sync.dma_start(last_raw[:, first:stop], x_rows[:, 3, first:stop])
         s_rows = w_scales.rearrange("e a q n -> q (e a) n")
         for q in range(4):
             nc.sync.dma_start(w_bytes[32 * q : 32 * q + 4, :, :].bitcast(I32), s_rows[4 * q : 4 * q + 4, :, :].bitcast(I32))
         w_rows = w_words.rearrange("e a p n r -> p (e a) (n r)").bitcast(I32)
-        nc.sync.dma_start(w_codes[0][:].bitcast(I32), w_rows[:, : E // 2, :])
+        nc.sync.dma_start(w_first[:].bitcast(I32), w_rows[:, : E // 2, :])
         nc.sync.dma_start(bias[:], b)
-        first_weight = keep.tile([P, widths[0]], F32, name="first_weight")
-        nc.sync.dma_start(first_weight[:], gate[:, : widths[0]])
+        nc.sync.dma_start(gate_first[:], gate[:, :CHUNK])
 
         nc.vector.memset(warm[:], 0.0)
         nc.gpsimd.memset(window[:], 0.0)
         nc.scalar.activation(warm[:], warm[:], SILU)
 
         def listed(c):
-            return offsets[:, chunks[c].start * C // 16 : chunks[c].stop * C // 16]
+            return offsets[:, c * CHUNK // 16 : (c + 1) * CHUNK // 16]
 
-        def cast(kind, first, last, share):
-            src = raw[kind, first][:].rearrange("p t n -> p n t")
-            dst = {"pair": pairs[:], "first": first_plane[:].unsqueeze(2), "last": last_plane[:].unsqueeze(2)}[kind]
+        def cast_plane(plane, raw, first, stop, share):
             if share > 0:
-                nc.scalar.copy(dst[:, first : first + share, :], src[:, :share, :])
-            other = nc.gpsimd if kind == "last" else nc.vector
-            other.tensor_copy(dst[:, first + share : last, :], src[:, share:, :])
+                nc.scalar.copy(plane[:, first : first + share], raw[:, first : first + share])
+            nc.gpsimd.tensor_copy(plane[:, first + share : stop], raw[:, first + share : stop])
+
+        def place(t, c):
+            return grouped[c][:].rearrange("p (n t) -> p n t", t=PACK)[:, :, t]
 
         def gather_pair(c):
             words = pairs[:].rearrange("p n t -> p (n t)").bitcast(U32)
-            into = grouped[c].bitcast(U32).rearrange("p (n u) -> p n u", u=2)[:, :, 0]
+            into = grouped[c][:].bitcast(U32).rearrange("p (n u) -> p n u", u=2)[:, :, 0]
             nc.vector.tensor_copy(into, words.indirect(listed(c)))
 
-        def gather_plane(plane, t, c):
-            into = grouped[c].rearrange("p (n t) -> p n t", t=PACK)[:, :, t]
-            nc.scalar.activation(into, plane[:].indirect(listed(c)), COPY)
+        def gather_vector(raw, t, c):
+            nc.vector.tensor_copy(place(t, c), raw[:].indirect(listed(c)))
 
-        def multiply(c):
-            width = len(chunks[c]) * C
-            codes = keep.tile([P, width], U32, name=f"codes{c}", align_bytes=64)
-            scales = keep.tile([P, width], U8, name=f"scales{c}", align_bytes=64)
-            if c > 0:
-                nc.vector.quantize_mx(out=codes[:].bitcast(FP8X4), scales=scales[:], in_=grouped[c])
-            for i, e in enumerate(chunks[c]):
+        def gather_scalar(plane, t, c):
+            nc.scalar.activation(place(t, c), plane[:].indirect(listed(c)), COPY)
+
+        def multiply(c, parts):
+            codes = keep.tile([P, CHUNK], U32, name=f"codes{c}", align_bytes=64)
+            scales = keep.tile([P, CHUNK], U8, name=f"scales{c}", align_bytes=64)
+            step = CHUNK // parts
+            for first in range(0, CHUNK, step):
+                nc.vector.quantize_mx(
+                    out=codes[:, first : first + step].bitcast(FP8X4),
+                    scales=scales[:, first : first + step],
+                    in_=grouped[c][:, PACK * first : PACK * (first + step)],
+                )
+            for i in range(CHUNK // C):
+                e = c * (CHUNK // C) + i
                 cols = slice(i * C, (i + 1) * C)
-                if c == 0:
-                    nc.vector.quantize_mx(
-                        out=codes[:, cols].bitcast(FP8X4),
-                        scales=scales[:, cols],
-                        in_=grouped[c][:, PACK * cols.start : PACK * cols.stop],
-                    )
                 nc.tensor.matmul_mx(
                     out=banks[e][:],
                     lhsT=w_codes[e // 4][:, e % 4, :].bitcast(FP8X4),
@@ -123,36 +122,47 @@ def tile_moe_res_lin_silu_kernel(tc, xT, xr, w_words, w_scales, b, gate, offs, o
                 nc.scalar.activation(y[c][:, cols], banks[e][:], SILU, bias=bias[:, e : e + 1])
 
         def scatter(c):
-            nc.vector.tensor_tensor(window[:].indirect(listed(c)), y[c], weight[c], MULT)
+            nc.vector.tensor_tensor(window[:].indirect(listed(c)), y[c][:], weight[c], MULT)
 
-        for load in LOADS[:2]:
-            cast(*load)
-        for c in range(len(chunks)):
-            gather_plane(first_plane, 2, c)
-        for load in LOADS[2:]:
-            cast(*load)
-        nc.sync.dma_start(again[0][:], last_plane[:])
-        w_codes.append(keep.tile([P, E // 2, N], U32, name="w_late", align_bytes=64))
-        nc.sync.dma_start(w_codes[1][:].bitcast(I32), w_rows[:, E // 2 :, :])
-        late = keep.tile([P, SLOTS - widths[0] + T], F32, name="late", tag=f"rawlast{LOADS[-1][1]}")
-        weight = [first_weight[:]] + [late[:, i * widths[1] : (i + 1) * widths[1]] for i in range(3)]
-        residual = late[:, SLOTS - widths[0] :]
-        nc.sync.dma_start(late[:, : SLOTS - widths[0]], gate[:, widths[0] :])
-        nc.sync.dma_start(again[1][:], last_plane[:])
+        for raw, (first, stop, share) in zip(pair_raw, PAIR_PIECES):
+            src = raw[:].rearrange("p t n -> p n t")
+            nc.scalar.copy(pairs[:, first : first + share, :], src[:, :share, :])
+            nc.vector.tensor_copy(pairs[:, first + share : stop, :], src[:, share:, :])
+        for c in range(CHUNKS):
+            gather_pair(c)
+        for piece in THIRD_PIECES:
+            cast_plane(third, third_raw, *piece)
+        gather_vector(third_raw, 2, 0)
+        gather_scalar(third, 2, 1)
+        gather_scalar(third, 2, 2)
+        for piece in LAST_PIECES:
+            cast_plane(last, last_raw, *piece)
+        gather_vector(last_raw, 3, 0)
+        gather_scalar(last, 3, 1)
+
+        nc.sync.dma_start(last_again[:], last[:])
+        third_again = turns.tile([P, T], BF16, name="third_again", offset=0, align_bytes=64)
+        w_second = turns.tile([P, E // 2, N], U32, name="w_second", offset=8192, align_bytes=64)
+        late = turns.tile([P, SLOTS - CHUNK + T], F32, name="late", offset=10240, align_bytes=64)
+        w_codes = [w_first, w_second]
+        weight = [gate_first[:]] + [late[:, i * CHUNK : (i + 1) * CHUNK] for i in range(CHUNKS - 1)]
+        residual = late[:, SLOTS - CHUNK :]
+        nc.sync.dma_start(w_second[:].bitcast(I32), w_rows[:, E // 2 :, :])
+        nc.sync.dma_start(weight[1], gate[:, CHUNK : 2 * CHUNK])
+        nc.sync.dma_start(third_again[:], third[:])
+        nc.sync.dma_start(late[:, CHUNK : SLOTS - CHUNK], gate[:, 2 * CHUNK :])
         for i in range(2):
             nc.sync.dma_start(residual[:, i * (T // 2) : (i + 1) * (T // 2)], xr[:, i * (T // 2) : (i + 1) * (T // 2)])
-        for c in range(len(chunks)):
-            gather_pair(c)
-        gather_plane(last_plane, 3, 0)
-        gather_plane(last_plane, 3, 1)
-        multiply(0)
-        gather_plane(again[0], 3, 2)
-        multiply(1)
+
+        multiply(0, 2)
+        multiply(1, 1)
+        gather_scalar(last_again, 3, 2)
         scatter(0)
-        gather_plane(again[1], 3, 3)
-        multiply(2)
+        gather_scalar(last_again, 3, 3)
+        gather_scalar(third_again, 2, 3)
+        multiply(2, 1)
         scatter(1)
-        multiply(3)
+        multiply(3, 1)
         scatter(2)
         scatter(3)
 

@@ -25,7 +25,7 @@ CHUNKS = SLOTS // CHUNK
 PAIR_PIECES = ((0, 1536, 512), (1536, 2816, 448), (2816, 3584, 256), (3584, 4096, 160))
 THIRD_PIECES = ((0, 1536, 896), (1536, 2816, 768), (2816, 3584, 448), (3584, 4096, 320))
 LAST_PIECES = ((0, 512, 0), (512, 1536, 0), (1536, 2560, 0), (2560, 3584, 640), (3584, 4096, 320))
-STORE_WIDTHS = (256, 384, 512, 704, 896, 832, 512)
+STORE_WIDTHS = (320, 384, 448, 512, 576, 640, 704, 512)
 
 
 def tile_moe_res_lin_silu_kernel(tc, xT, xr, w_words, w_scales, b, gate, offs, out):
@@ -140,7 +140,8 @@ def tile_moe_res_lin_silu_kernel(tc, xT, xr, w_words, w_scales, b, gate, offs, o
         gather_vector(last_raw, 3, 0)
         gather_scalar(last, 3, 1)
 
-        nc.sync.dma_start(last_again[:], last[:])
+        for first, stop in ((0, 2560), (2560, T)):
+            nc.sync.dma_start(last_again[:, first:stop], last[:, first:stop])
         third_again = turns.tile([P, T], BF16, name="third_again", offset=0, align_bytes=64)
         w_second = turns.tile([P, E // 2, N], U32, name="w_second", offset=8192, align_bytes=64)
         late = turns.tile([P, SLOTS - CHUNK + T], F32, name="late", offset=10240, align_bytes=64)

@@ -22,6 +22,7 @@ P = 128
 PACK = 4
 CHUNK = 2 * C
 CHUNKS = SLOTS // CHUNK
+MERGED = (3,)
 PAIR_PIECES = ((0, 1536, 512), (1536, 2816, 448), (2816, 3584, 256), (3584, 4096, 160))
 THIRD_PIECES = ((0, 1536, 896), (1536, 2816, 768), (2816, 3584, 448), (3584, 4096, 320))
 LAST_PIECES = ((0, 512, 0), (512, 1536, 0), (1536, 2560, 0), (2560, 3584, 640), (3584, 4096, 320))
@@ -47,6 +48,7 @@ def tile_moe_res_lin_silu_kernel(tc, xT, xr, w_words, w_scales, b, gate, offs, o
         bias = keep.tile([P, E], F32, name="bias")
         gate_first = keep.tile([P, CHUNK], F32, name="gate_first")
         grouped = [keep.tile([P, PACK * CHUNK], BF16, name=f"grouped{c}", align_bytes=64) for c in range(CHUNKS)]
+        halves = {c: keep.tile([P, 2, CHUNK], U32, name=f"halves{c}", align_bytes=64) for c in MERGED}
         y = [keep.tile([P, CHUNK], F32, name=f"y{c}") for c in range(CHUNKS)]
         window = keep.tile([P, T], F32, name="window")
         warm = keep.tile([P, 1], F32, name="warm")
@@ -84,11 +86,15 @@ def tile_moe_res_lin_silu_kernel(tc, xT, xr, w_words, w_scales, b, gate, offs, o
             nc.gpsimd.tensor_copy(plane[:, first + share : stop], raw[:, first + share : stop])
 
         def place(t, c):
+            if c in MERGED:
+                return halves[c][:, 1, :].bitcast(BF16).rearrange("p (n t) -> p n t", t=2)[:, :, t - 2]
             return grouped[c][:].rearrange("p (n t) -> p n t", t=PACK)[:, :, t]
 
         def gather_pair(c):
             words = pairs[:].rearrange("p n t -> p (n t)").bitcast(U32)
             into = grouped[c][:].bitcast(U32).rearrange("p (n u) -> p n u", u=2)[:, :, 0]
+            if c in MERGED:
+                into = halves[c][:, 0, :]
             nc.vector.tensor_copy(into, words.indirect(listed(c)))
 
         def gather_vector(raw, t, c):
@@ -96,6 +102,10 @@ def tile_moe_res_lin_silu_kernel(tc, xT, xr, w_words, w_scales, b, gate, offs, o
 
         def gather_scalar(plane, t, c):
             nc.scalar.activation(place(t, c), plane[:].indirect(listed(c)), COPY)
+
+        def merge(c):
+            into = grouped[c][:].bitcast(U32).rearrange("p (n u) -> p n u", u=2)
+            nc.scalar.copy(into, halves[c][:].rearrange("p u n -> p n u"))
 
         def multiply(c, parts):
             codes = keep.tile([P, CHUNK], U32, name=f"codes{c}", align_bytes=64)
@@ -148,12 +158,12 @@ def tile_moe_res_lin_silu_kernel(tc, xT, xr, w_words, w_scales, b, gate, offs, o
         w_codes = [w_first, w_second]
         weight = [gate_first[:]] + [late[:, i * CHUNK : (i + 1) * CHUNK] for i in range(CHUNKS - 1)]
         residual = late[:, SLOTS - CHUNK :]
+        nc.sync.dma_start(third_again[:], third[:])
         nc.sync.dma_start(w_second[:].bitcast(I32), w_rows[:, E // 2 :, :])
         nc.sync.dma_start(weight[1], gate[:, CHUNK : 2 * CHUNK])
-        nc.sync.dma_start(third_again[:], third[:])
+        nc.sync.dma_start(residual[:, : T // 2], xr[:, : T // 2])
         nc.sync.dma_start(late[:, CHUNK : SLOTS - CHUNK], gate[:, 2 * CHUNK :])
-        for i in range(2):
-            nc.sync.dma_start(residual[:, i * (T // 2) : (i + 1) * (T // 2)], xr[:, i * (T // 2) : (i + 1) * (T // 2)])
+        nc.sync.dma_start(residual[:, T // 2 :], xr[:, T // 2 :])
 
         multiply(0, 2)
         multiply(1, 1)
@@ -161,6 +171,7 @@ def tile_moe_res_lin_silu_kernel(tc, xT, xr, w_words, w_scales, b, gate, offs, o
         scatter(0)
         gather_scalar(last_again, 3, 3)
         gather_scalar(third_again, 2, 3)
+        merge(3)
         multiply(2, 1)
         scatter(1)
         multiply(3, 1)

@@ -23,7 +23,7 @@ PACK = 4
 CHUNK = 2 * C
 CHUNKS = SLOTS // CHUNK
 MERGED = (3,)
-PAIR_PIECES = ((0, 1536, 512), (1536, 2816, 448), (2816, 3584, 256), (3584, 4096, 160))
+PAIR_PIECES = ((0, 1472, 480), (1472, 2624, 384), (2624, 3520, 288), (3520, 4096, 192))
 THIRD_PIECES = ((0, 1536, 896), (1536, 2816, 768), (2816, 3584, 448), (3584, 4096, 320))
 LAST_PIECES = ((0, 512, 0), (512, 1536, 0), (1536, 2560, 0), (2560, 3584, 640), (3584, 4096, 320))
 STORE_WIDTHS = (320, 384, 448, 512, 576, 640, 704, 512)
@@ -40,12 +40,12 @@ def tile_moe_res_lin_silu_kernel(tc, xT, xr, w_words, w_scales, b, gate, offs, o
         pairs = keep.tile([P, T, 2], BF16, name="pairs", align_bytes=64)
         third_raw = keep.tile([P, T], F32, name="third_raw")
         third = keep.tile([P, T], BF16, name="third", align_bytes=64)
-        last_raw = turns.tile([P, T], F32, name="last_raw", offset=8128, align_bytes=64)
+        last_raw = turns.tile([P, T], F32, name="last_raw", offset=0, align_bytes=64)
         last = keep.tile([P, T], BF16, name="last", align_bytes=64)
         last_again = keep.tile([P, T], BF16, name="last_again", align_bytes=64)
-        w_first = keep.tile([P, E // 2, N], U32, name="w_first", align_bytes=64)
+        w_first = keep.tile([P, 2, N], U32, name="w_first", align_bytes=64)
         w_bytes = keep.tile([P, E, N], U8, name="w_bytes", align_bytes=64)
-        bias = keep.tile([P, E], F32, name="bias")
+        bias_late = keep.tile([P, E // 2], F32, name="bias_late")
         gate_first = keep.tile([P, CHUNK], F32, name="gate_first")
         grouped = [keep.tile([P, PACK * CHUNK], BF16, name=f"grouped{c}", align_bytes=64) for c in range(CHUNKS)]
         halves = {c: keep.tile([P, 2, CHUNK], U32, name=f"halves{c}", align_bytes=64) for c in MERGED}
@@ -57,10 +57,10 @@ def tile_moe_res_lin_silu_kernel(tc, xT, xr, w_words, w_scales, b, gate, offs, o
         nc.vector.memset(w_bytes[:].bitcast(I32), 0)
         nc.sync.dma_start(offsets[:], offs)
         x_rows = xT.rearrange("(p t) w -> p t w", t=PACK)
-        pair_raw = []
+        pair_raw = keep.tile([P, 2, T], F32, name="pair_raw")
+        nc.sync.dma_start(pair_raw[:, 0, :], x_rows[:, 0, :])
         for first, stop, share in PAIR_PIECES:
-            pair_raw.append(keep.tile([P, 2, stop - first], F32, name=f"pair_raw{first}"))
-            nc.sync.dma_start(pair_raw[-1][:], x_rows[:, 0:2, first:stop])
+            nc.sync.dma_start(pair_raw[:, 1, first:stop], x_rows[:, 1, first:stop])
         for first, stop, share in THIRD_PIECES:
             nc.sync.dma_start(third_raw[:, first:stop], x_rows[:, 2, first:stop])
         for first, stop, share in LAST_PIECES:
@@ -69,8 +69,9 @@ def tile_moe_res_lin_silu_kernel(tc, xT, xr, w_words, w_scales, b, gate, offs, o
         for q in range(4):
             nc.sync.dma_start(w_bytes[32 * q : 32 * q + 4, :, :].bitcast(I32), s_rows[4 * q : 4 * q + 4, :, :].bitcast(I32))
         w_rows = w_words.rearrange("e a p n r -> p (e a) (n r)").bitcast(I32)
-        nc.sync.dma_start(w_first[:].bitcast(I32), w_rows[:, : E // 2, :])
-        nc.sync.dma_start(bias[:], b)
+        nc.sync.dma_start(w_first[:].bitcast(I32), w_rows[:, :2, :])
+        bias_first = halves[3][:, 1, : E // 2].bitcast(F32)
+        nc.sync.dma_start(bias_first, b[:, : E // 2])
         nc.sync.dma_start(gate_first[:], gate[:, :CHUNK])
 
         nc.vector.memset(warm[:], 0.0)
@@ -105,7 +106,9 @@ def tile_moe_res_lin_silu_kernel(tc, xT, xr, w_words, w_scales, b, gate, offs, o
 
         def merge(c):
             into = grouped[c][:].bitcast(U32).rearrange("p (n u) -> p n u", u=2)
-            nc.scalar.copy(into, halves[c][:].rearrange("p u n -> p n u"))
+            rows = halves[c][:].rearrange("p u n -> p n u")
+            for first in range(0, CHUNK, C):
+                nc.scalar.copy(into[:, first : first + C, :], rows[:, first : first + C, :])
 
         def multiply(c, parts):
             codes = keep.tile([P, CHUNK], U32, name=f"codes{c}", align_bytes=64)
@@ -122,22 +125,22 @@ def tile_moe_res_lin_silu_kernel(tc, xT, xr, w_words, w_scales, b, gate, offs, o
                 cols = slice(i * C, (i + 1) * C)
                 nc.tensor.matmul_mx(
                     out=banks[e][:],
-                    lhsT=w_codes[e // 4][:, e % 4, :].bitcast(FP8X4),
+                    lhsT=w_codes[e].bitcast(FP8X4),
                     lhsT_scale=w_bytes[:, e, :],
                     rhs=codes[:, cols].bitcast(FP8X4),
                     rhs_scale=scales[:, cols],
                     start=True,
                     stop=True,
                 )
-                nc.scalar.activation(y[c][:, cols], banks[e][:], SILU, bias=bias[:, e : e + 1])
+                nc.scalar.activation(y[c][:, cols], banks[e][:], SILU, bias=(bias_first, bias_late)[e // 4][:, e % 4 : e % 4 + 1])
 
         def scatter(c):
             nc.vector.tensor_tensor(window[:].indirect(listed(c)), y[c][:], weight[c], MULT)
 
-        for raw, (first, stop, share) in zip(pair_raw, PAIR_PIECES):
-            src = raw[:].rearrange("p t n -> p n t")
-            nc.scalar.copy(pairs[:, first : first + share, :], src[:, :share, :])
-            nc.vector.tensor_copy(pairs[:, first + share : stop, :], src[:, share:, :])
+        src = pair_raw[:].rearrange("p t n -> p n t")
+        for first, stop, share in PAIR_PIECES:
+            nc.scalar.copy(pairs[:, first : first + share, :], src[:, first : first + share, :])
+            nc.vector.tensor_copy(pairs[:, first + share : stop, :], src[:, first + share : stop, :])
         for c in range(CHUNKS):
             gather_pair(c)
         for piece in THIRD_PIECES:
@@ -152,29 +155,29 @@ def tile_moe_res_lin_silu_kernel(tc, xT, xr, w_words, w_scales, b, gate, offs, o
 
         for first, stop in ((0, 2560), (2560, T)):
             nc.sync.dma_start(last_again[:, first:stop], last[:, first:stop])
-        third_again = turns.tile([P, T], BF16, name="third_again", offset=0, align_bytes=64)
-        w_second = turns.tile([P, E // 2, N], U32, name="w_second", offset=8192, align_bytes=64)
+        w_second = turns.tile([P, E - 2, N], U32, name="w_second", offset=7168, align_bytes=64)
         late = turns.tile([P, SLOTS - CHUNK + T], F32, name="late", offset=10240, align_bytes=64)
-        w_codes = [w_first, w_second]
+        w_codes = [w_first[:, e, :] for e in range(2)] + [w_second[:, e, :] for e in range(E - 2)]
         weight = [gate_first[:]] + [late[:, i * CHUNK : (i + 1) * CHUNK] for i in range(CHUNKS - 1)]
         residual = late[:, SLOTS - CHUNK :]
-        nc.sync.dma_start(third_again[:], third[:])
-        nc.sync.dma_start(w_second[:].bitcast(I32), w_rows[:, E // 2 :, :])
+        nc.sync.dma_start(w_second[:, :2, :].bitcast(I32), w_rows[:, 2:4, :])
         nc.sync.dma_start(weight[1], gate[:, CHUNK : 2 * CHUNK])
-        nc.sync.dma_start(residual[:, : T // 2], xr[:, : T // 2])
+        nc.sync.dma_start(w_second[:, 2:, :].bitcast(I32), w_rows[:, 4:, :])
+        nc.sync.dma_start(bias_late[:], b[:, E // 2 :])
+        nc.sync.dma_start(residual[:, : 3 * T // 4], xr[:, : 3 * T // 4])
         nc.sync.dma_start(late[:, CHUNK : SLOTS - CHUNK], gate[:, 2 * CHUNK :])
-        nc.sync.dma_start(residual[:, T // 2 :], xr[:, T // 2 :])
+        nc.sync.dma_start(residual[:, 3 * T // 4 :], xr[:, 3 * T // 4 :])
 
         multiply(0, 2)
-        multiply(1, 1)
         gather_scalar(last_again, 3, 2)
+        multiply(1, 1)
         scatter(0)
-        gather_scalar(last_again, 3, 3)
-        gather_scalar(third_again, 2, 3)
+        gather_scalar(third, 2, 3)
+        gather_scalar(last, 3, 3)
         merge(3)
         multiply(2, 1)
         scatter(1)
-        multiply(3, 1)
+        multiply(3, 2)
         scatter(2)
         scatter(3)
 

@@ -22,11 +22,16 @@ P = 128
 PACK = 4
 CHUNK = 2 * C
 CHUNKS = SLOTS // CHUNK
-MERGED = (3,)
+LAST_CHUNK = CHUNKS - 1
+FIRST_EXPERTS = CHUNK // C
+
 PAIR_PIECES = ((0, 1472, 480), (1472, 2624, 384), (2624, 3520, 288), (3520, 4096, 192))
 THIRD_PIECES = ((0, 1536, 896), (1536, 2816, 768), (2816, 3584, 448), (3584, 4096, 320))
-LAST_PIECES = ((0, 512, 0), (512, 1536, 0), (1536, 2560, 0), (2560, 3584, 640), (3584, 4096, 320))
+LAST_PIECES = ((0, 512, 0), (512, 1536, 0), (1536, 2816, 0), (2816, 3584, 448), (3584, 4096, 320))
+VECTOR_PIECE = 2
+EARLY_COLUMNS = LAST_PIECES[3][0]
 STORE_WIDTHS = (320, 384, 448, 512, 576, 640, 704, 512)
+TABLE_COLUMNS = 8
 
 
 def tile_moe_res_lin_silu_kernel(tc, xT, xr, w_words, w_scales, b, gate, offs, out):
@@ -43,16 +48,14 @@ def tile_moe_res_lin_silu_kernel(tc, xT, xr, w_words, w_scales, b, gate, offs, o
         last_raw = turns.tile([P, T], F32, name="last_raw", offset=0, align_bytes=64)
         last = keep.tile([P, T], BF16, name="last", align_bytes=64)
         last_again = keep.tile([P, T], BF16, name="last_again", align_bytes=64)
-        w_first = keep.tile([P, 2, N], U32, name="w_first", align_bytes=64)
+        w_first = keep.tile([P, FIRST_EXPERTS, N], U32, name="w_first", align_bytes=64)
         w_bytes = keep.tile([P, E, N], U8, name="w_bytes", align_bytes=64)
         bias_late = keep.tile([P, E // 2], F32, name="bias_late")
         gate_first = keep.tile([P, CHUNK], F32, name="gate_first")
         grouped = [keep.tile([P, PACK * CHUNK], BF16, name=f"grouped{c}", align_bytes=64) for c in range(CHUNKS)]
-        halves = {c: keep.tile([P, 2, CHUNK], U32, name=f"halves{c}", align_bytes=64) for c in MERGED}
+        halves = keep.tile([P, 2, CHUNK], U32, name="halves", align_bytes=64)
         y = [keep.tile([P, CHUNK], F32, name=f"y{c}") for c in range(CHUNKS)]
         window = keep.tile([P, T], F32, name="window")
-        warm = keep.tile([P, 1], F32, name="warm")
-        banks = [psum.tile([P, C], F32, name=f"bank{e}") for e in range(E)]
 
         nc.vector.memset(w_bytes[:].bitcast(I32), 0)
         nc.sync.dma_start(offsets[:], offs)
@@ -69,34 +72,35 @@ def tile_moe_res_lin_silu_kernel(tc, xT, xr, w_words, w_scales, b, gate, offs, o
         for q in range(4):
             nc.sync.dma_start(w_bytes[32 * q : 32 * q + 4, :, :].bitcast(I32), s_rows[4 * q : 4 * q + 4, :, :].bitcast(I32))
         w_rows = w_words.rearrange("e a p n r -> p (e a) (n r)").bitcast(I32)
-        nc.sync.dma_start(w_first[:].bitcast(I32), w_rows[:, :2, :])
-        bias_first = halves[3][:, 1, : E // 2].bitcast(F32)
+        nc.sync.dma_start(w_first[:].bitcast(I32), w_rows[:, :FIRST_EXPERTS, :])
+        bias_first = halves[:, 1, : E // 2].bitcast(F32)
         nc.sync.dma_start(bias_first, b[:, : E // 2])
         nc.sync.dma_start(gate_first[:], gate[:, :CHUNK])
 
-        nc.vector.memset(warm[:], 0.0)
-        nc.gpsimd.memset(window[:], 0.0)
-        nc.scalar.activation(warm[:], warm[:], SILU)
+        nc.vector.memset(window[:, :TABLE_COLUMNS], 0.0)
+        nc.gpsimd.memset(window[:, TABLE_COLUMNS:], 0.0)
+        nc.scalar.activation(window[:, :TABLE_COLUMNS], window[:, :TABLE_COLUMNS], SILU)
 
         def listed(c):
             return offsets[:, c * CHUNK // 16 : (c + 1) * CHUNK // 16]
 
-        def cast_plane(plane, raw, first, stop, share):
+        def cast_piece(plane, raw, first, stop, share, other):
             if share > 0:
                 nc.scalar.copy(plane[:, first : first + share], raw[:, first : first + share])
-            nc.gpsimd.tensor_copy(plane[:, first + share : stop], raw[:, first + share : stop])
+            other.tensor_copy(plane[:, first + share : stop], raw[:, first + share : stop])
 
         def place(t, c):
-            if c in MERGED:
-                return halves[c][:, 1, :].bitcast(BF16).rearrange("p (n t) -> p n t", t=2)[:, :, t - 2]
+            if c == LAST_CHUNK:
+                return halves[:, 1, :].bitcast(BF16).rearrange("p (n t) -> p n t", t=2)[:, :, t - 2]
             return grouped[c][:].rearrange("p (n t) -> p n t", t=PACK)[:, :, t]
 
+        def slot_words(c):
+            return grouped[c][:].bitcast(U32).rearrange("p (n u) -> p n u", u=2)
+
         def gather_pair(c):
-            words = pairs[:].rearrange("p n t -> p (n t)").bitcast(U32)
-            into = grouped[c][:].bitcast(U32).rearrange("p (n u) -> p n u", u=2)[:, :, 0]
-            if c in MERGED:
-                into = halves[c][:, 0, :]
-            nc.vector.tensor_copy(into, words.indirect(listed(c)))
+            token_words = pairs[:].rearrange("p n t -> p (n t)").bitcast(U32)
+            into = halves[:, 0, :] if c == LAST_CHUNK else slot_words(c)[:, :, 0]
+            nc.vector.tensor_copy(into, token_words.indirect(listed(c)))
 
         def gather_vector(raw, t, c):
             nc.vector.tensor_copy(place(t, c), raw[:].indirect(listed(c)))
@@ -104,27 +108,28 @@ def tile_moe_res_lin_silu_kernel(tc, xT, xr, w_words, w_scales, b, gate, offs, o
         def gather_scalar(plane, t, c):
             nc.scalar.activation(place(t, c), plane[:].indirect(listed(c)), COPY)
 
-        def merge(c):
-            into = grouped[c][:].bitcast(U32).rearrange("p (n u) -> p n u", u=2)
-            rows = halves[c][:].rearrange("p u n -> p n u")
+        def merge_halves():
+            rows = halves[:].rearrange("p u n -> p n u")
             for first in range(0, CHUNK, C):
-                nc.scalar.copy(into[:, first : first + C, :], rows[:, first : first + C, :])
+                nc.scalar.copy(slot_words(LAST_CHUNK)[:, first : first + C, :], rows[:, first : first + C, :])
 
-        def multiply(c, parts):
+        def multiply(c, starts):
             codes = keep.tile([P, CHUNK], U32, name=f"codes{c}", align_bytes=64)
             scales = keep.tile([P, CHUNK], U8, name=f"scales{c}", align_bytes=64)
-            step = CHUNK // parts
-            for first in range(0, CHUNK, step):
+            edges = list(starts) + [CHUNK]
+            for first, stop in zip(edges, edges[1:]):
                 nc.vector.quantize_mx(
-                    out=codes[:, first : first + step].bitcast(FP8X4),
-                    scales=scales[:, first : first + step],
-                    in_=grouped[c][:, PACK * first : PACK * (first + step)],
+                    out=codes[:, first:stop].bitcast(FP8X4),
+                    scales=scales[:, first:stop],
+                    in_=grouped[c][:, PACK * first : PACK * stop],
                 )
-            for i in range(CHUNK // C):
-                e = c * (CHUNK // C) + i
-                cols = slice(i * C, (i + 1) * C)
+            edges = sorted(set(edges) | {C})
+            for first, stop in zip(edges, edges[1:]):
+                e = (c * CHUNK + first) // C
+                cols = slice(first, stop)
+                bank = psum.tile([P, stop - first], F32, name="bank", tag="bank", bufs=E)
                 nc.tensor.matmul_mx(
-                    out=banks[e][:],
+                    out=bank[:],
                     lhsT=w_codes[e].bitcast(FP8X4),
                     lhsT_scale=w_bytes[:, e, :],
                     rhs=codes[:, cols].bitcast(FP8X4),
@@ -132,58 +137,60 @@ def tile_moe_res_lin_silu_kernel(tc, xT, xr, w_words, w_scales, b, gate, offs, o
                     start=True,
                     stop=True,
                 )
-                nc.scalar.activation(y[c][:, cols], banks[e][:], SILU, bias=(bias_first, bias_late)[e // 4][:, e % 4 : e % 4 + 1])
+                nc.scalar.activation(y[c][:, cols], bank[:], SILU, bias=bias[e])
 
         def scatter(c):
             nc.vector.tensor_tensor(window[:].indirect(listed(c)), y[c][:], weight[c], MULT)
 
-        src = pair_raw[:].rearrange("p t n -> p n t")
+        both = pair_raw[:].rearrange("p t n -> p n t")
         for first, stop, share in PAIR_PIECES:
-            nc.scalar.copy(pairs[:, first : first + share, :], src[:, first : first + share, :])
-            nc.vector.tensor_copy(pairs[:, first + share : stop, :], src[:, first + share : stop, :])
+            nc.scalar.copy(pairs[:, first : first + share, :], both[:, first : first + share, :])
+            nc.vector.tensor_copy(pairs[:, first + share : stop, :], both[:, first + share : stop, :])
         for c in range(CHUNKS):
             gather_pair(c)
         for piece in THIRD_PIECES:
-            cast_plane(third, third_raw, *piece)
+            cast_piece(third, third_raw, *piece, nc.gpsimd)
         gather_vector(third_raw, 2, 0)
         gather_scalar(third, 2, 1)
         gather_scalar(third, 2, 2)
-        for piece in LAST_PIECES:
-            cast_plane(last, last_raw, *piece)
+        for i, piece in enumerate(LAST_PIECES):
+            cast_piece(last, last_raw, *piece, nc.vector if i == VECTOR_PIECE else nc.gpsimd)
         gather_vector(last_raw, 3, 0)
         gather_scalar(last, 3, 1)
 
-        for first, stop in ((0, 2560), (2560, T)):
+        for first, stop in ((0, EARLY_COLUMNS), (EARLY_COLUMNS, T)):
             nc.sync.dma_start(last_again[:, first:stop], last[:, first:stop])
-        w_second = turns.tile([P, E - 2, N], U32, name="w_second", offset=7168, align_bytes=64)
-        late = turns.tile([P, SLOTS - CHUNK + T], F32, name="late", offset=10240, align_bytes=64)
-        w_codes = [w_first[:, e, :] for e in range(2)] + [w_second[:, e, :] for e in range(E - 2)]
+        late_at = 10240
+        w_late = turns.tile([P, E - FIRST_EXPERTS, N], U32, name="w_late", offset=late_at - 4 * N * (E - FIRST_EXPERTS), align_bytes=64)
+        late = turns.tile([P, SLOTS - CHUNK + T], F32, name="late", offset=late_at, align_bytes=64)
+        w_codes = [w_first[:, e, :] for e in range(FIRST_EXPERTS)] + [w_late[:, e, :] for e in range(E - FIRST_EXPERTS)]
+        bias = [half[:, e : e + 1] for half in (bias_first, bias_late) for e in range(E // 2)]
         weight = [gate_first[:]] + [late[:, i * CHUNK : (i + 1) * CHUNK] for i in range(CHUNKS - 1)]
         residual = late[:, SLOTS - CHUNK :]
-        nc.sync.dma_start(w_second[:, :2, :].bitcast(I32), w_rows[:, 2:4, :])
+        nc.sync.dma_start(w_late[:, :FIRST_EXPERTS, :].bitcast(I32), w_rows[:, FIRST_EXPERTS : E // 2, :])
         nc.sync.dma_start(weight[1], gate[:, CHUNK : 2 * CHUNK])
-        nc.sync.dma_start(w_second[:, 2:, :].bitcast(I32), w_rows[:, 4:, :])
+        nc.sync.dma_start(w_late[:, FIRST_EXPERTS:, :].bitcast(I32), w_rows[:, E // 2 :, :])
         nc.sync.dma_start(bias_late[:], b[:, E // 2 :])
         nc.sync.dma_start(residual[:, : 3 * T // 4], xr[:, : 3 * T // 4])
         nc.sync.dma_start(late[:, CHUNK : SLOTS - CHUNK], gate[:, 2 * CHUNK :])
         nc.sync.dma_start(residual[:, 3 * T // 4 :], xr[:, 3 * T // 4 :])
 
-        multiply(0, 2)
+        multiply(0, (0, C // 2, C))
         gather_scalar(last_again, 3, 2)
-        multiply(1, 1)
+        multiply(1, (0,))
         scatter(0)
-        gather_scalar(third, 2, 3)
-        gather_scalar(last, 3, 3)
-        merge(3)
-        multiply(2, 1)
+        gather_scalar(third, 2, LAST_CHUNK)
+        gather_scalar(last, 3, LAST_CHUNK)
+        merge_halves()
+        multiply(2, (0,))
         scatter(1)
-        multiply(3, 2)
+        multiply(LAST_CHUNK, (0, C))
         scatter(2)
-        scatter(3)
+        scatter(LAST_CHUNK)
 
-        start = 0
+        first = 0
         for i, width in enumerate(STORE_WIDTHS):
             res = keep.tile([P, width], F32, name=f"res{i}")
-            nc.vector.tensor_tensor(res[:], window[:, start : start + width], residual[:, start : start + width], ADD)
-            nc.sync.dma_start(out[:, start : start + width], res[:])
-            start += width
+            nc.vector.tensor_tensor(res[:], window[:, first : first + width], residual[:, first : first + width], ADD)
+            nc.sync.dma_start(out[:, first : first + width], res[:])
+            first += width

@@ -22,14 +22,7 @@ P = 128
 PACK = 4
 CHUNK = 2 * C
 CHUNKS = SLOTS // CHUNK
-LAST_CHUNK = CHUNKS - 1
-FIRST_EXPERTS = CHUNK // C
-
-PAIR_PIECES = ((0, 1472, 480), (1472, 2624, 384), (2624, 3520, 288), (3520, 4096, 192))
-THIRD_PIECES = ((0, 1536, 896), (1536, 2816, 768), (2816, 3584, 448), (3584, 4096, 320))
-LAST_PIECES = ((0, 512, 0), (512, 1536, 0), (1536, 2816, 0), (2816, 3584, 448), (3584, 4096, 320))
-VECTOR_PIECE = 2
-EARLY_COLUMNS = LAST_PIECES[3][0]
+PER_CHUNK = CHUNK // C
 STORE_WIDTHS = (320, 384, 448, 512, 576, 640, 704, 512)
 TABLE_COLUMNS = 8
 
@@ -38,155 +31,127 @@ def tile_moe_res_lin_silu_kernel(tc, xT, xr, w_words, w_scales, b, gate, offs, o
     nc = tc.nc
     with ExitStack() as ctx:
         keep = ctx.enter_context(tc.tile_pool(name="keep", bufs=1))
-        turns = ctx.enter_context(tc.tile_pool(name="turns", bufs=1))
         psum = ctx.enter_context(tc.psum_pool(name="psum", bufs=1))
 
         offsets = keep.tile([P, SLOTS // 16], U16, name="offsets")
-        pairs = keep.tile([P, T, 2], BF16, name="pairs", align_bytes=64)
-        third_raw = keep.tile([P, T], F32, name="third_raw")
-        third = keep.tile([P, T], BF16, name="third", align_bytes=64)
-        last_raw = turns.tile([P, T], F32, name="last_raw", offset=0, align_bytes=64)
-        last = keep.tile([P, T], BF16, name="last", align_bytes=64)
-        last_again = keep.tile([P, T], BF16, name="last_again", align_bytes=64)
-        w_first = keep.tile([P, FIRST_EXPERTS, N], U32, name="w_first", align_bytes=64)
+        planes = [keep.tile([P, T], F32, name=f"plane{t}") for t in range(PACK)]
+        w_codes = [keep.tile([P, PER_CHUNK, N], U32, name=f"w_codes{c}", align_bytes=64) for c in range(CHUNKS)]
         w_bytes = keep.tile([P, E, N], U8, name="w_bytes", align_bytes=64)
-        bias_late = keep.tile([P, E // 2], F32, name="bias_late")
-        gate_first = keep.tile([P, CHUNK], F32, name="gate_first")
         grouped = [keep.tile([P, PACK * CHUNK], BF16, name=f"grouped{c}", align_bytes=64) for c in range(CHUNKS)]
-        halves = keep.tile([P, 2, CHUNK], U32, name="halves", align_bytes=64)
-        y = [keep.tile([P, CHUNK], F32, name=f"y{c}") for c in range(CHUNKS)]
+        early = {c: keep.tile([P, 2 * CHUNK], BF16, name=f"early{c}") for c in (2, 3)}
+        late = {c: keep.tile([P, 2 * CHUNK], BF16, name=f"late{c}") for c in (1, 2, 3)}
+        y_ends = [keep.tile([P, CHUNK], F32, name=f"y_end{i}") for i in range(2)]
+        y = [y_ends[0][:], late[2][:].bitcast(F32), late[3][:].bitcast(F32), y_ends[1][:]]
+        bias_rest = keep.tile([P, E // 2], F32, name="bias_rest")
+        bias_parked = [late[c + 2][:, CHUNK + C - 2 : CHUNK + C + 2].bitcast(F32) for c in range(2)]
+        bias = [bias_parked[e // 2][:, e % 2 : e % 2 + 1] for e in range(E // 2)] + [bias_rest[:, e : e + 1] for e in range(E // 2)]
+        gates = [keep.tile([P, CHUNK], F32, name=f"gate{c}") for c in range(CHUNKS)]
+        residual = keep.tile([P, T], F32, name="residual")
         window = keep.tile([P, T], F32, name="window")
 
-        nc.vector.memset(w_bytes[:].bitcast(I32), 0)
+        nc.gpsimd.memset(w_bytes[:].bitcast(I32), 0)
         nc.sync.dma_start(offsets[:], offs)
         x_rows = xT.rearrange("(p t) w -> p t w", t=PACK)
-        pair_raw = keep.tile([P, 2, T], F32, name="pair_raw")
-        nc.sync.dma_start(pair_raw[:, 0, :], x_rows[:, 0, :])
-        for first, stop, share in PAIR_PIECES:
-            nc.sync.dma_start(pair_raw[:, 1, first:stop], x_rows[:, 1, first:stop])
-        for first, stop, share in THIRD_PIECES:
-            nc.sync.dma_start(third_raw[:, first:stop], x_rows[:, 2, first:stop])
-        for first, stop, share in LAST_PIECES:
-            nc.sync.dma_start(last_raw[:, first:stop], x_rows[:, 3, first:stop])
+        for t in range(PACK):
+            nc.sync.dma_start(planes[t][:], x_rows[:, t, :])
         s_rows = w_scales.rearrange("e a q n -> q (e a) n")
         for q in range(4):
             nc.sync.dma_start(w_bytes[32 * q : 32 * q + 4, :, :].bitcast(I32), s_rows[4 * q : 4 * q + 4, :, :].bitcast(I32))
         w_rows = w_words.rearrange("e a p n r -> p (e a) (n r)").bitcast(I32)
-        nc.sync.dma_start(w_first[:].bitcast(I32), w_rows[:, :FIRST_EXPERTS, :])
-        bias_first = halves[:, 1, : E // 2].bitcast(F32)
-        nc.sync.dma_start(bias_first, b[:, : E // 2])
-        nc.sync.dma_start(gate_first[:], gate[:, :CHUNK])
+        for c in range(CHUNKS):
+            experts = slice(c * PER_CHUNK, (c + 1) * PER_CHUNK)
+            nc.sync.dma_start(w_codes[c][:].bitcast(I32), w_rows[:, experts, :])
+            if c < 2:
+                nc.sync.dma_start(bias_parked[c], b[:, experts])
+            if c == 2:
+                nc.sync.dma_start(bias_rest[:], b[:, E // 2 :])
+            nc.sync.dma_start(gates[c][:], gate[:, c * CHUNK : (c + 1) * CHUNK])
+        nc.sync.dma_start(residual[:], xr)
 
         nc.vector.memset(window[:, :TABLE_COLUMNS], 0.0)
         nc.gpsimd.memset(window[:, TABLE_COLUMNS:], 0.0)
         nc.scalar.activation(window[:, :TABLE_COLUMNS], window[:, :TABLE_COLUMNS], SILU)
 
-        def listed(c):
-            return offsets[:, c * CHUNK // 16 : (c + 1) * CHUNK // 16]
+        def listed(c, first=0, stop=CHUNK):
+            return offsets[:, (c * CHUNK + first) // 16 : (c * CHUNK + stop) // 16]
 
-        def cast_piece(plane, raw, first, stop, share, other):
-            if share > 0:
-                nc.scalar.copy(plane[:, first : first + share], raw[:, first : first + share])
-            other.tensor_copy(plane[:, first + share : stop], raw[:, first + share : stop])
+        def slots(c):
+            return grouped[c][:].rearrange("p (n t) -> p n t", t=PACK)
 
-        def place(t, c):
-            if c == LAST_CHUNK:
-                return halves[:, 1, :].bitcast(BF16).rearrange("p (n t) -> p n t", t=2)[:, :, t - 2]
-            return grouped[c][:].rearrange("p (n t) -> p n t", t=PACK)[:, :, t]
+        def gather_placed(t, c):
+            nc.vector.tensor_copy(slots(c)[:, :, t], planes[t][:].indirect(listed(c)))
 
-        def slot_words(c):
-            return grouped[c][:].bitcast(U32).rearrange("p (n u) -> p n u", u=2)
+        def gather_row(engine, t, c, first=0, stop=CHUNK):
+            rows = early[c] if t < 2 else late[c]
+            into = rows[:, (t % 2) * CHUNK + first : (t % 2) * CHUNK + stop]
+            if engine is nc.scalar:
+                nc.scalar.activation(into, planes[t][:].indirect(listed(c, first, stop)), COPY)
+            else:
+                nc.vector.tensor_copy(into, planes[t][:].indirect(listed(c, first, stop)))
 
-        def gather_pair(c):
-            token_words = pairs[:].rearrange("p n t -> p (n t)").bitcast(U32)
-            into = halves[:, 0, :] if c == LAST_CHUNK else slot_words(c)[:, :, 0]
-            nc.vector.tensor_copy(into, token_words.indirect(listed(c)))
+        def weave(copy, rows, u, c, first=0, stop=CHUNK):
+            copy(slots(c)[:, first:stop, 2 * u : 2 * u + 2], rows[:].rearrange("p (t n) -> p n t", t=2)[:, first:stop, :])
 
-        def gather_vector(raw, t, c):
-            nc.vector.tensor_copy(place(t, c), raw[:].indirect(listed(c)))
+        codes = [keep.tile([P, CHUNK], U32, name=f"codes{c}", align_bytes=64) for c in range(CHUNKS)]
+        scales = [keep.tile([P, CHUNK], U8, name=f"scales{c}", align_bytes=64) for c in range(CHUNKS)]
 
-        def gather_scalar(plane, t, c):
-            nc.scalar.activation(place(t, c), plane[:].indirect(listed(c)), COPY)
-
-        def merge_halves():
-            rows = halves[:].rearrange("p u n -> p n u")
-            for first in range(0, CHUNK, C):
-                nc.scalar.copy(slot_words(LAST_CHUNK)[:, first : first + C, :], rows[:, first : first + C, :])
-
-        def multiply(c, starts):
-            codes = keep.tile([P, CHUNK], U32, name=f"codes{c}", align_bytes=64)
-            scales = keep.tile([P, CHUNK], U8, name=f"scales{c}", align_bytes=64)
-            edges = list(starts) + [CHUNK]
+        def quantise(c, edges):
             for first, stop in zip(edges, edges[1:]):
                 nc.vector.quantize_mx(
-                    out=codes[:, first:stop].bitcast(FP8X4),
-                    scales=scales[:, first:stop],
+                    out=codes[c][:, first:stop].bitcast(FP8X4),
+                    scales=scales[c][:, first:stop],
                     in_=grouped[c][:, PACK * first : PACK * stop],
                 )
-            edges = sorted(set(edges) | {C})
+
+        def multiply(c, edges):
             for first, stop in zip(edges, edges[1:]):
                 e = (c * CHUNK + first) // C
                 cols = slice(first, stop)
                 bank = psum.tile([P, stop - first], F32, name="bank", tag="bank", bufs=E)
                 nc.tensor.matmul_mx(
                     out=bank[:],
-                    lhsT=w_codes[e].bitcast(FP8X4),
+                    lhsT=w_codes[c][:, e % PER_CHUNK, :].bitcast(FP8X4),
                     lhsT_scale=w_bytes[:, e, :],
-                    rhs=codes[:, cols].bitcast(FP8X4),
-                    rhs_scale=scales[:, cols],
+                    rhs=codes[c][:, cols].bitcast(FP8X4),
+                    rhs_scale=scales[c][:, cols],
                     start=True,
                     stop=True,
                 )
                 nc.scalar.activation(y[c][:, cols], bank[:], SILU, bias=bias[e])
 
         def scatter(c):
-            nc.vector.tensor_tensor(window[:].indirect(listed(c)), y[c][:], weight[c], MULT)
+            nc.vector.tensor_tensor(window[:].indirect(listed(c)), y[c], gates[c][:], MULT)
 
-        both = pair_raw[:].rearrange("p t n -> p n t")
-        for first, stop, share in PAIR_PIECES:
-            nc.scalar.copy(pairs[:, first : first + share, :], both[:, first : first + share, :])
-            nc.vector.tensor_copy(pairs[:, first + share : stop, :], both[:, first + share : stop, :])
-        for c in range(CHUNKS):
-            gather_pair(c)
-        for piece in THIRD_PIECES:
-            cast_piece(third, third_raw, *piece, nc.gpsimd)
-        gather_vector(third_raw, 2, 0)
-        gather_scalar(third, 2, 1)
-        gather_scalar(third, 2, 2)
-        for i, piece in enumerate(LAST_PIECES):
-            cast_piece(last, last_raw, *piece, nc.vector if i == VECTOR_PIECE else nc.gpsimd)
-        gather_vector(last_raw, 3, 0)
-        gather_scalar(last, 3, 1)
+        for t in range(2):
+            gather_placed(t, 0)
+            gather_placed(t, 1)
+            gather_row(nc.scalar, t, 3)
+            gather_row(nc.scalar, t, 2)
+        weave(nc.vector.tensor_copy, early[3], 0, 3)
+        weave(nc.scalar.copy, early[2], 0, 2)
+        gather_placed(2, 0)
+        gather_row(nc.vector, 2, 3)
+        gather_row(nc.scalar, 2, 1)
+        gather_row(nc.scalar, 2, 2)
 
-        for first, stop in ((0, EARLY_COLUMNS), (EARLY_COLUMNS, T)):
-            nc.sync.dma_start(last_again[:, first:stop], last[:, first:stop])
-        late_at = 10240
-        w_late = turns.tile([P, E - FIRST_EXPERTS, N], U32, name="w_late", offset=late_at - 4 * N * (E - FIRST_EXPERTS), align_bytes=64)
-        late = turns.tile([P, SLOTS - CHUNK + T], F32, name="late", offset=late_at, align_bytes=64)
-        w_codes = [w_first[:, e, :] for e in range(FIRST_EXPERTS)] + [w_late[:, e, :] for e in range(E - FIRST_EXPERTS)]
-        bias = [half[:, e : e + 1] for half in (bias_first, bias_late) for e in range(E // 2)]
-        weight = [gate_first[:]] + [late[:, i * CHUNK : (i + 1) * CHUNK] for i in range(CHUNKS - 1)]
-        residual = late[:, SLOTS - CHUNK :]
-        nc.sync.dma_start(w_late[:, :FIRST_EXPERTS, :].bitcast(I32), w_rows[:, FIRST_EXPERTS : E // 2, :])
-        nc.sync.dma_start(weight[1], gate[:, CHUNK : 2 * CHUNK])
-        nc.sync.dma_start(w_late[:, FIRST_EXPERTS:, :].bitcast(I32), w_rows[:, E // 2 :, :])
-        nc.sync.dma_start(bias_late[:], b[:, E // 2 :])
-        nc.sync.dma_start(residual[:, : 3 * T // 4], xr[:, : 3 * T // 4])
-        nc.sync.dma_start(late[:, CHUNK : SLOTS - CHUNK], gate[:, 2 * CHUNK :])
-        nc.sync.dma_start(residual[:, 3 * T // 4 :], xr[:, 3 * T // 4 :])
-
-        multiply(0, (0, C // 2, C))
-        gather_scalar(last_again, 3, 2)
-        multiply(1, (0,))
+        gather_placed(3, 0)
+        gather_row(nc.scalar, 3, 1)
+        quantise(0, (0, C // 2, C, CHUNK))
+        for first in (0, C):
+            weave(nc.vector.tensor_copy, late[1], 1, 1, first, first + C)
+        quantise(1, (0, C, CHUNK))
+        multiply(0, (0, C // 2, C, CHUNK))
         scatter(0)
-        gather_scalar(third, 2, LAST_CHUNK)
-        gather_scalar(last, 3, LAST_CHUNK)
-        merge_halves()
-        multiply(2, (0,))
-        scatter(1)
-        multiply(LAST_CHUNK, (0, C))
-        scatter(2)
-        scatter(LAST_CHUNK)
+        for c in (2, 3):
+            for first in (0, C):
+                gather_row(nc.scalar, 3, c, first, first + C)
+            for first in (0, C):
+                weave(nc.scalar.copy, late[c], 1, c, first, first + C)
+            quantise(c, (0, CHUNK))
+            multiply(c - 1, (0, C, CHUNK))
+            scatter(c - 1)
+        multiply(3, (0, C, CHUNK))
+        scatter(3)
 
         first = 0
         for i, width in enumerate(STORE_WIDTHS):

@@ -39,7 +39,7 @@ def tile_moe_res_lin_silu_kernel(tc, xT, xr, w_words, w_scales, b, gate, offs, o
         w_bytes = keep.tile([P, E, N], U8, name="w_bytes", align_bytes=64)
         grouped = [keep.tile([P, PACK * CHUNK], BF16, name=f"grouped{c}", align_bytes=64) for c in range(CHUNKS)]
         early = {c: keep.tile([P, 2 * CHUNK], BF16, name=f"early{c}") for c in (2, 3)}
-        late = {c: keep.tile([P, 2 * CHUNK], BF16, name=f"late{c}") for c in (1, 2, 3)}
+        late = {c: keep.tile([P, 2 * CHUNK], BF16, name=f"late{c}") for c in range(CHUNKS)}
         y_ends = [keep.tile([P, CHUNK], F32, name=f"y_end{i}") for i in range(2)]
         y = [y_ends[0][:], late[2][:].bitcast(F32), late[3][:].bitcast(F32), y_ends[1][:]]
         bias_rest = keep.tile([P, E // 2], F32, name="bias_rest")
@@ -129,18 +129,29 @@ def tile_moe_res_lin_silu_kernel(tc, xT, xr, w_words, w_scales, b, gate, offs, o
             gather_row(nc.scalar, t, 2)
         weave(nc.vector.tensor_copy, early[3], 0, 3)
         weave(nc.scalar.copy, early[2], 0, 2)
-        gather_placed(2, 0)
+        gather_row(nc.vector, 2, 0)
         gather_row(nc.vector, 2, 3)
         gather_row(nc.scalar, 2, 1)
         gather_row(nc.scalar, 2, 2)
 
-        gather_placed(3, 0)
-        gather_row(nc.scalar, 3, 1)
-        quantise(0, (0, C // 2, C, CHUNK))
+        gather_row(nc.vector, 3, 0, 0, C // 2)
+        gather_row(nc.vector, 3, 0, C // 2, C)
+        gather_row(nc.scalar, 3, 0, C, CHUNK)
         for first in (0, C):
-            weave(nc.vector.tensor_copy, late[1], 1, 1, first, first + C)
+            gather_row(nc.scalar, 3, 1, first, first + C)
+        weave(nc.scalar.copy, late[1], 1, 1, 0, C // 2)
+        part = C // 2
+        weave(nc.vector.tensor_copy, late[0], 1, 0, 0, part)
+        for first in range(0, CHUNK, part):
+            following = first + part
+            if following < CHUNK:
+                weave(nc.vector.tensor_copy, late[0], 1, 0, following, following + part)
+            else:
+                weave(nc.vector.tensor_copy, late[1], 1, 1, part, C)
+            quantise(0, (first, following))
+        weave(nc.vector.tensor_copy, late[1], 1, 1, C, CHUNK)
         quantise(1, (0, C, CHUNK))
-        multiply(0, (0, C // 2, C, CHUNK))
+        multiply(0, range(0, CHUNK + 1, part))
         scatter(0)
         for c in (2, 3):
             for first in (0, C):

@@ -23,6 +23,8 @@ PACK = 4
 CHUNK = 2 * C
 CHUNKS = SLOTS // CHUNK
 PER_CHUNK = CHUNK // C
+PART = C // 2
+HELD = (2, 3)
 STORE_WIDTHS = (320, 384, 448, 512, 576, 640, 704, 512)
 TABLE_COLUMNS = 8
 
@@ -38,13 +40,14 @@ def tile_moe_res_lin_silu_kernel(tc, xT, xr, w_words, w_scales, b, gate, offs, o
         w_codes = [keep.tile([P, PER_CHUNK, N], U32, name=f"w_codes{c}", align_bytes=64) for c in range(CHUNKS)]
         w_bytes = keep.tile([P, E, N], U8, name="w_bytes", align_bytes=64)
         grouped = [keep.tile([P, PACK * CHUNK], BF16, name=f"grouped{c}", align_bytes=64) for c in range(CHUNKS)]
-        early = {c: keep.tile([P, 2 * CHUNK], BF16, name=f"early{c}") for c in (2, 3)}
+        early = {c: keep.tile([P, 2 * CHUNK], BF16, name=f"early{c}") for c in HELD}
         late = {c: keep.tile([P, 2 * CHUNK], BF16, name=f"late{c}") for c in range(CHUNKS)}
         y_ends = [keep.tile([P, CHUNK], F32, name=f"y_end{i}") for i in range(2)]
         y = [y_ends[0][:], late[2][:].bitcast(F32), late[3][:].bitcast(F32), y_ends[1][:]]
         bias_rest = keep.tile([P, E // 2], F32, name="bias_rest")
-        bias_parked = [late[c + 2][:, CHUNK + C - 2 : CHUNK + C + 2].bitcast(F32) for c in range(2)]
-        bias = [bias_parked[e // 2][:, e % 2 : e % 2 + 1] for e in range(E // 2)] + [bias_rest[:, e : e + 1] for e in range(E // 2)]
+        bias_parked = [late[c][:, CHUNK + C - 2 : CHUNK + C + 2].bitcast(F32) for c in HELD]
+        bias = [half[:, e : e + 1] for half in bias_parked for e in range(PER_CHUNK)]
+        bias.extend(bias_rest[:, e : e + 1] for e in range(E // 2))
         gates = [keep.tile([P, CHUNK], F32, name=f"gate{c}") for c in range(CHUNKS)]
         residual = keep.tile([P, T], F32, name="residual")
         window = keep.tile([P, T], F32, name="window")
@@ -61,9 +64,9 @@ def tile_moe_res_lin_silu_kernel(tc, xT, xr, w_words, w_scales, b, gate, offs, o
         for c in range(CHUNKS):
             experts = slice(c * PER_CHUNK, (c + 1) * PER_CHUNK)
             nc.sync.dma_start(w_codes[c][:].bitcast(I32), w_rows[:, experts, :])
-            if c < 2:
+            if c < len(bias_parked):
                 nc.sync.dma_start(bias_parked[c], b[:, experts])
-            if c == 2:
+            if c == len(bias_parked):
                 nc.sync.dma_start(bias_rest[:], b[:, E // 2 :])
             nc.sync.dma_start(gates[c][:], gate[:, c * CHUNK : (c + 1) * CHUNK])
         nc.sync.dma_start(residual[:], xr)
@@ -81,16 +84,19 @@ def tile_moe_res_lin_silu_kernel(tc, xT, xr, w_words, w_scales, b, gate, offs, o
         def gather_placed(t, c):
             nc.vector.tensor_copy(slots(c)[:, :, t], planes[t][:].indirect(listed(c)))
 
-        def gather_row(engine, t, c, first=0, stop=CHUNK):
+        def row(t, c, first, stop):
             rows = early[c] if t < 2 else late[c]
-            into = rows[:, (t % 2) * CHUNK + first : (t % 2) * CHUNK + stop]
-            if engine is nc.scalar:
-                nc.scalar.activation(into, planes[t][:].indirect(listed(c, first, stop)), COPY)
-            else:
-                nc.vector.tensor_copy(into, planes[t][:].indirect(listed(c, first, stop)))
+            return rows[:, (t % 2) * CHUNK + first : (t % 2) * CHUNK + stop]
 
-        def weave(copy, rows, u, c, first=0, stop=CHUNK):
-            copy(slots(c)[:, first:stop, 2 * u : 2 * u + 2], rows[:].rearrange("p (t n) -> p n t", t=2)[:, first:stop, :])
+        def gather_vector(t, c, first=0, stop=CHUNK):
+            nc.vector.tensor_copy(row(t, c, first, stop), planes[t][:].indirect(listed(c, first, stop)))
+
+        def gather_scalar(t, c, first=0, stop=CHUNK):
+            nc.scalar.activation(row(t, c, first, stop), planes[t][:].indirect(listed(c, first, stop)), COPY)
+
+        def weave(copy, t, c, first=0, stop=CHUNK):
+            rows = early[c] if t < 2 else late[c]
+            copy(slots(c)[:, first:stop, t : t + 2], rows[:].rearrange("p (t n) -> p n t", t=2)[:, first:stop, :])
 
         codes = [keep.tile([P, CHUNK], U32, name=f"codes{c}", align_bytes=64) for c in range(CHUNKS)]
         scales = [keep.tile([P, CHUNK], U8, name=f"scales{c}", align_bytes=64) for c in range(CHUNKS)]
@@ -122,47 +128,49 @@ def tile_moe_res_lin_silu_kernel(tc, xT, xr, w_words, w_scales, b, gate, offs, o
         def scatter(c):
             nc.vector.tensor_tensor(window[:].indirect(listed(c)), y[c], gates[c][:], MULT)
 
+        on_vector, on_scalar = nc.vector.tensor_copy, nc.scalar.copy
+        halves = (0, C, CHUNK)
+
         for t in range(2):
             gather_placed(t, 0)
             gather_placed(t, 1)
-            gather_row(nc.scalar, t, 3)
-            gather_row(nc.scalar, t, 2)
-        weave(nc.vector.tensor_copy, early[3], 0, 3)
-        weave(nc.scalar.copy, early[2], 0, 2)
-        gather_row(nc.vector, 2, 0)
-        gather_row(nc.vector, 2, 3)
-        gather_row(nc.scalar, 2, 1)
-        gather_row(nc.scalar, 2, 2)
+            gather_scalar(t, 3)
+            gather_scalar(t, 2)
+        weave(on_vector, 0, 3)
+        weave(on_scalar, 0, 2)
+        gather_vector(2, 0)
+        gather_vector(2, 3)
+        gather_scalar(2, 1)
+        gather_scalar(2, 2)
 
-        gather_row(nc.vector, 3, 0, 0, C // 2)
-        gather_row(nc.vector, 3, 0, C // 2, C)
-        gather_row(nc.scalar, 3, 0, C, CHUNK)
+        gather_vector(3, 0, 0, PART)
+        gather_vector(3, 0, PART, C)
+        gather_scalar(3, 0, C, CHUNK)
         for first in (0, C):
-            gather_row(nc.scalar, 3, 1, first, first + C)
-        weave(nc.scalar.copy, late[1], 1, 1, 0, C // 2)
-        part = C // 2
-        weave(nc.vector.tensor_copy, late[0], 1, 0, 0, part)
-        for first in range(0, CHUNK, part):
-            following = first + part
-            if following < CHUNK:
-                weave(nc.vector.tensor_copy, late[0], 1, 0, following, following + part)
-            else:
-                weave(nc.vector.tensor_copy, late[1], 1, 1, part, C)
-            quantise(0, (first, following))
-        weave(nc.vector.tensor_copy, late[1], 1, 1, C, CHUNK)
-        quantise(1, (0, C, CHUNK))
-        multiply(0, range(0, CHUNK + 1, part))
+            gather_scalar(3, 1, first, first + C)
+        weave(on_scalar, 2, 1, 0, PART)
+        last_part = CHUNK - PART
+        for first in range(0, last_part, PART):
+            weave(on_vector, 2, 0, first, first + PART)
+        quantise(0, (0, PART))
+        weave(on_vector, 2, 0, last_part, CHUNK)
+        quantise(0, range(PART, CHUNK + 1, PART))
+        weave(on_vector, 2, 1, PART, C)
+        weave(on_vector, 2, 1, C, CHUNK)
+        quantise(1, halves)
+        multiply(0, range(0, CHUNK + 1, PART))
         scatter(0)
-        for c in (2, 3):
+
+        for c in HELD:
             for first in (0, C):
-                gather_row(nc.scalar, 3, c, first, first + C)
+                gather_scalar(3, c, first, first + C)
             for first in (0, C):
-                weave(nc.scalar.copy, late[c], 1, c, first, first + C)
+                weave(on_scalar, 2, c, first, first + C)
             quantise(c, (0, CHUNK))
-            multiply(c - 1, (0, C, CHUNK))
+            multiply(c - 1, halves)
             scatter(c - 1)
-        multiply(3, (0, C, CHUNK))
-        scatter(3)
+        multiply(CHUNKS - 1, halves)
+        scatter(CHUNKS - 1)
 
         first = 0
         for i, width in enumerate(STORE_WIDTHS):

@@ -25,7 +25,7 @@ CHUNKS = SLOTS // CHUNK
 PER_CHUNK = CHUNK // C
 PART = C // 2
 HELD = (2, 3)
-STORE_WIDTHS = (320, 384, 448, 512, 576, 640, 704, 512)
+STORE_WIDTHS = (256, 320, 384, 464, 544, 624, 704, 800)
 TABLE_COLUMNS = 8
 
 
@@ -52,7 +52,7 @@ def tile_moe_res_lin_silu_kernel(tc, xT, xr, w_words, w_scales, b, gate, offs, o
         residual = keep.tile([P, T], F32, name="residual")
         window = keep.tile([P, T], F32, name="window")
 
-        nc.gpsimd.memset(w_bytes[:].bitcast(I32), 0)
+        nc.vector.memset(w_bytes[:].bitcast(I32), 0)
         nc.sync.dma_start(offsets[:], offs)
         x_rows = xT.rearrange("(p t) w -> p t w", t=PACK)
         for t in range(PACK):
@@ -72,7 +72,7 @@ def tile_moe_res_lin_silu_kernel(tc, xT, xr, w_words, w_scales, b, gate, offs, o
         nc.sync.dma_start(residual[:], xr)
 
         nc.vector.memset(window[:, :TABLE_COLUMNS], 0.0)
-        nc.gpsimd.memset(window[:, TABLE_COLUMNS:], 0.0)
+        nc.vector.memset(window[:, TABLE_COLUMNS:], 0.0)
         nc.scalar.activation(window[:, :TABLE_COLUMNS], window[:, :TABLE_COLUMNS], SILU)
 
         def listed(c, first=0, stop=CHUNK):

@@ -1,6 +1,7 @@
 from contextlib import ExitStack
 
 import concourse.mybir as mybir
+from concourse.masks import make_identity
 
 K, T, E, C, N = 512, 4096, 8, 256, 128
 SLOTS = E * C
@@ -25,8 +26,11 @@ CHUNKS = SLOTS // CHUNK
 PER_CHUNK = CHUNK // C
 PART = C // 2
 HELD = (2, 3)
-STORE_WIDTHS = (256, 320, 384, 464, 544, 624, 704, 800)
+ADD_WIDTHS = (192, 288, 384, 480, 576, 672, 480)
+UNIT = 2 * P
+UNITS = (T - sum(ADD_WIDTHS)) // UNIT
 TABLE_COLUMNS = 8
+BANKS = 4
 
 
 def tile_moe_res_lin_silu_kernel(tc, xT, xr, w_words, w_scales, b, gate, offs, out):
@@ -51,11 +55,14 @@ def tile_moe_res_lin_silu_kernel(tc, xT, xr, w_words, w_scales, b, gate, offs, o
         gates = [keep.tile([P, CHUNK], F32, name=f"gate{c}") for c in range(CHUNKS)]
         residual = keep.tile([P, T], F32, name="residual")
         window = keep.tile([P, T], F32, name="window")
+        identity = keep.tile([P, P], F32, name="identity")
+        make_identity(nc, identity[:])
 
         nc.vector.memset(w_bytes[:].bitcast(I32), 0)
-        nc.sync.dma_start(offsets[:], offs)
         x_rows = xT.rearrange("(p t) w -> p t w", t=PACK)
-        for t in range(PACK):
+        nc.sync.dma_start(planes[0][:], x_rows[:, 0, :])
+        nc.sync.dma_start(offsets[:], offs)
+        for t in range(1, PACK):
             nc.sync.dma_start(planes[t][:], x_rows[:, t, :])
         s_rows = w_scales.rearrange("e a q n -> q (e a) n")
         for q in range(4):
@@ -113,7 +120,7 @@ def tile_moe_res_lin_silu_kernel(tc, xT, xr, w_words, w_scales, b, gate, offs, o
             for first, stop in zip(edges, edges[1:]):
                 e = (c * CHUNK + first) // C
                 cols = slice(first, stop)
-                bank = psum.tile([P, stop - first], F32, name="bank", tag="bank", bufs=E)
+                bank = psum.tile([P, stop - first], F32, name="bank", tag="bank", bufs=BANKS)
                 nc.tensor.matmul_mx(
                     out=bank[:],
                     lhsT=w_codes[c][:, e % PER_CHUNK, :].bitcast(FP8X4),
@@ -170,11 +177,37 @@ def tile_moe_res_lin_silu_kernel(tc, xT, xr, w_words, w_scales, b, gate, offs, o
             multiply(c - 1, halves)
             scatter(c - 1)
         multiply(CHUNKS - 1, halves)
+
+        shared = sum(ADD_WIDTHS)
+        sums = [psum.tile([P, UNIT], F32, name=f"sum{u}") for u in range(UNITS)]
+
+        def turn_onto(u, source, opens):
+            for h in range(2):
+                first = shared + u * UNIT + h * P
+                nc.tensor.matmul(
+                    sums[u][:, h * P : (h + 1) * P], source[:, first : first + P], identity[:],
+                    start=opens and h == 0, stop=not opens and h == 1, is_transpose=True,
+                )
+
+        for u in range(UNITS):
+            turn_onto(u, residual, True)
         scatter(CHUNKS - 1)
 
+        turned = [keep.tile([P, UNIT], F32, name=f"turned{u}") for u in range(UNITS)]
+        for u in range(UNITS):
+            turn_onto(u, window, False)
+            nc.scalar.copy(turned[u][:], sums[u][:])
+        last = keep.tile([P, ADD_WIDTHS[-1] + T - shared], F32, name="last")
+        for u in range(UNITS):
+            back = psum.tile([P, UNIT], F32, name="back", tag="bank", bufs=BANKS)
+            for h in range(2):
+                nc.tensor.transpose(back[:, h * P : (h + 1) * P], turned[u][:, h * P : (h + 1) * P], identity[:])
+            at = ADD_WIDTHS[-1] + u * UNIT
+            nc.scalar.copy(last[:, at : at + UNIT], back[:])
+
         first = 0
-        for i, width in enumerate(STORE_WIDTHS):
-            res = keep.tile([P, width], F32, name=f"res{i}")
-            nc.vector.tensor_tensor(res[:], window[:, first : first + width], residual[:, first : first + width], ADD)
-            nc.sync.dma_start(out[:, first : first + width], res[:])
+        for i, width in enumerate(ADD_WIDTHS):
+            res = last if i == len(ADD_WIDTHS) - 1 else keep.tile([P, width], F32, name=f"res{i}")
+            nc.vector.tensor_tensor(res[:, :width], window[:, first : first + width], residual[:, first : first + width], ADD)
+            nc.sync.dma_start(out[:, first : first + res.shape[1]], res[:])
             first += width

@@ -1,7 +1,6 @@
 from contextlib import ExitStack
 
 import concourse.mybir as mybir
-from concourse.masks import make_identity
 
 K, T, E, C, N = 512, 4096, 8, 256, 128
 SLOTS = E * C
@@ -16,6 +15,7 @@ U8 = mybir.dt.uint8
 FP8X4 = mybir.dt.float8_e4m3fn_x4
 MULT = mybir.AluOpType.mult
 ADD = mybir.AluOpType.add
+EQUAL = mybir.AluOpType.is_equal
 COPY = mybir.ActivationFunctionType.Copy
 SILU = mybir.ActivationFunctionType.Silu
 
@@ -56,7 +56,6 @@ def tile_moe_res_lin_silu_kernel(tc, xT, xr, w_words, w_scales, b, gate, offs, o
         residual = keep.tile([P, T], F32, name="residual")
         window = keep.tile([P, T], F32, name="window")
         identity = keep.tile([P, P], F32, name="identity")
-        make_identity(nc, identity[:])
 
         nc.vector.memset(w_bytes[:].bitcast(I32), 0)
         x_rows = xT.rearrange("(p t) w -> p t w", t=PACK)
@@ -77,6 +76,15 @@ def tile_moe_res_lin_silu_kernel(tc, xT, xr, w_words, w_scales, b, gate, offs, o
                 nc.sync.dma_start(bias_rest[:], b[:, E // 2 :])
             nc.sync.dma_start(gates[c][:], gate[:, c * CHUNK : (c + 1) * CHUNK])
         nc.sync.dma_start(residual[:], xr)
+
+        ones = keep.tile([P, P], F32, name="ones")
+        column = keep.tile([P, P], F32, name="column", align_bytes=64)
+        turned_column = keep.tile([P, P], F32, name="turned_column", align_bytes=64)
+        nc.vector.memset(ones[:], 1.0)
+        nc.vector.tensor_tensor_scan(column[:], ones[:], ones[:], -1.0, MULT, ADD)
+        nc.vector.transpose(turned_column[:], column[:])
+        for q in range(0, P, 32):
+            nc.vector.tensor_scalar(identity[q : q + 32, :], column[q : q + 32, :], turned_column[q : q + 32, q : q + 1], None, EQUAL)
 
         nc.vector.memset(window[:, :TABLE_COLUMNS], 0.0)
         nc.vector.memset(window[:, TABLE_COLUMNS:], 0.0)

@@ -26,7 +26,7 @@ CHUNKS = SLOTS // CHUNK
 PER_CHUNK = CHUNK // C
 PART = C // 2
 HELD = (2, 3)
-ADD_WIDTHS = (192, 288, 384, 480, 576, 672, 480)
+ADD_WIDTHS = (264, 360, 456, 552, 664, 776)
 UNIT = 2 * P
 UNITS = (T - sum(ADD_WIDTHS)) // UNIT
 TABLE_COLUMNS = 8
@@ -205,17 +205,18 @@ def tile_moe_res_lin_silu_kernel(tc, xT, xr, w_words, w_scales, b, gate, offs, o
         for u in range(UNITS):
             turn_onto(u, window, False)
             nc.scalar.copy(turned[u][:], sums[u][:])
-        last = keep.tile([P, ADD_WIDTHS[-1] + T - shared], F32, name="last")
+        last = keep.tile([P, T - shared], F32, name="last")
         for u in range(UNITS):
             back = psum.tile([P, UNIT], F32, name="back", tag="bank", bufs=BANKS)
             for h in range(2):
                 nc.tensor.transpose(back[:, h * P : (h + 1) * P], turned[u][:, h * P : (h + 1) * P], identity[:])
-            at = ADD_WIDTHS[-1] + u * UNIT
+            at = u * UNIT
             nc.scalar.copy(last[:, at : at + UNIT], back[:])
 
         first = 0
         for i, width in enumerate(ADD_WIDTHS):
-            res = last if i == len(ADD_WIDTHS) - 1 else keep.tile([P, width], F32, name=f"res{i}")
-            nc.vector.tensor_tensor(res[:, :width], window[:, first : first + width], residual[:, first : first + width], ADD)
-            nc.sync.dma_start(out[:, first : first + res.shape[1]], res[:])
+            res = keep.tile([P, width], F32, name=f"res{i}")
+            nc.vector.tensor_tensor(res[:], window[:, first : first + width], residual[:, first : first + width], ADD)
+            nc.sync.dma_start(out[:, first : first + width], res[:])
             first += width
+        nc.sync.dma_start(out[:, shared:], last[:])

@@ -26,7 +26,7 @@ CHUNKS = SLOTS // CHUNK
 PER_CHUNK = CHUNK // C
 PART = C // 2
 HELD = (2, 3)
-ADD_WIDTHS = (264, 360, 456, 552, 664, 776)
+ADD_WIDTHS = (256, 384, 448, 576, 640, 768)
 UNIT = 2 * P
 UNITS = (T - sum(ADD_WIDTHS)) // UNIT
 TABLE_COLUMNS = 8
@@ -205,7 +205,7 @@ def tile_moe_res_lin_silu_kernel(tc, xT, xr, w_words, w_scales, b, gate, offs, o
         for u in range(UNITS):
             turn_onto(u, window, False)
             nc.scalar.copy(turned[u][:], sums[u][:])
-        last = keep.tile([P, T - shared], F32, name="last")
+        last = keep.tile([P, T - shared], F32, name="last", align_bytes=256)
         for u in range(UNITS):
             back = psum.tile([P, UNIT], F32, name="back", tag="bank", bufs=BANKS)
             for h in range(2):
@@ -215,7 +215,7 @@ def tile_moe_res_lin_silu_kernel(tc, xT, xr, w_words, w_scales, b, gate, offs, o
 
         first = 0
         for i, width in enumerate(ADD_WIDTHS):
-            res = keep.tile([P, width], F32, name=f"res{i}")
+            res = keep.tile([P, width], F32, name=f"res{i}", align_bytes=256)
             nc.vector.tensor_tensor(res[:], window[:, first : first + width], residual[:, first : first + width], ADD)
             nc.sync.dma_start(out[:, first : first + width], res[:])
             first += width

@@ -40,9 +40,9 @@ def tile_moe_res_lin_silu_kernel(tc, xT, xr, w_words, w_scales, b, gate, offs, o
         psum = ctx.enter_context(tc.psum_pool(name="psum", bufs=1))
 
         offsets = keep.tile([P, SLOTS // 16], U16, name="offsets")
-        planes = [keep.tile([P, T], F32, name=f"plane{t}") for t in range(PACK)]
-        w_codes = [keep.tile([P, PER_CHUNK, N], U32, name=f"w_codes{c}", align_bytes=64) for c in range(CHUNKS)]
-        w_bytes = keep.tile([P, E, N], U8, name="w_bytes", align_bytes=64)
+        planes = [keep.tile([P, T], F32, name=f"plane{t}", align_bytes=256) for t in range(PACK)]
+        w_codes = [keep.tile([P, PER_CHUNK, N], U32, name=f"w_codes{c}", align_bytes=256) for c in range(CHUNKS)]
+        w_bytes = keep.tile([P, E, N], U8, name="w_bytes", align_bytes=256)
         grouped = [keep.tile([P, PACK * CHUNK], BF16, name=f"grouped{c}", align_bytes=64) for c in range(CHUNKS)]
         early = {c: keep.tile([P, 2 * CHUNK], BF16, name=f"early{c}") for c in HELD}
         late = {c: keep.tile([P, 2 * CHUNK], BF16, name=f"late{c}") for c in range(CHUNKS)}
@@ -52,9 +52,9 @@ def tile_moe_res_lin_silu_kernel(tc, xT, xr, w_words, w_scales, b, gate, offs, o
         bias_parked = [late[c][:, CHUNK + C - 2 : CHUNK + C + 2].bitcast(F32) for c in HELD]
         bias = [half[:, e : e + 1] for half in bias_parked for e in range(PER_CHUNK)]
         bias.extend(bias_rest[:, e : e + 1] for e in range(E // 2))
-        gates = [keep.tile([P, CHUNK], F32, name=f"gate{c}") for c in range(CHUNKS)]
-        residual = keep.tile([P, T], F32, name="residual")
-        window = keep.tile([P, T], F32, name="window")
+        gates = [keep.tile([P, CHUNK], F32, name=f"gate{c}", align_bytes=256) for c in range(CHUNKS)]
+        residual = keep.tile([P, T], F32, name="residual", align_bytes=256)
+        window = keep.tile([P, T], F32, name="window", align_bytes=256)
         identity = keep.tile([P, P], F32, name="identity")
 
         nc.vector.memset(w_bytes[:].bitcast(I32), 0)

@@ -26,7 +26,7 @@ CHUNKS = SLOTS // CHUNK
 PER_CHUNK = CHUNK // C
 PART = C // 2
 HELD = (2, 3)
-ADD_WIDTHS = (256, 384, 448, 576, 640, 768)
+ADD_WIDTHS = (256, 384, 512, 512, 640, 768)
 UNIT = 2 * P
 UNITS = (T - sum(ADD_WIDTHS)) // UNIT
 TABLE_COLUMNS = 8
@@ -39,23 +39,23 @@ def tile_moe_res_lin_silu_kernel(tc, xT, xr, w_words, w_scales, b, gate, offs, o
         keep = ctx.enter_context(tc.tile_pool(name="keep", bufs=1))
         psum = ctx.enter_context(tc.psum_pool(name="psum", bufs=1))
 
-        offsets = keep.tile([P, SLOTS // 16], U16, name="offsets")
-        planes = [keep.tile([P, T], F32, name=f"plane{t}", align_bytes=256) for t in range(PACK)]
+        offsets = keep.tile([P, SLOTS // 16], U16, name="offsets", align_bytes=256)
+        planes = [keep.tile([P, T], F32, name=f"plane{t}", align_bytes=4096) for t in range(PACK)]
         w_codes = [keep.tile([P, PER_CHUNK, N], U32, name=f"w_codes{c}", align_bytes=256) for c in range(CHUNKS)]
         w_bytes = keep.tile([P, E, N], U8, name="w_bytes", align_bytes=256)
-        grouped = [keep.tile([P, PACK * CHUNK], BF16, name=f"grouped{c}", align_bytes=64) for c in range(CHUNKS)]
-        early = {c: keep.tile([P, 2 * CHUNK], BF16, name=f"early{c}") for c in HELD}
-        late = {c: keep.tile([P, 2 * CHUNK], BF16, name=f"late{c}") for c in range(CHUNKS)}
-        y_ends = [keep.tile([P, CHUNK], F32, name=f"y_end{i}") for i in range(2)]
+        grouped = [keep.tile([P, PACK * CHUNK], BF16, name=f"grouped{c}", align_bytes=256) for c in range(CHUNKS)]
+        early = {c: keep.tile([P, 2 * CHUNK], BF16, name=f"early{c}", align_bytes=256) for c in HELD}
+        late = {c: keep.tile([P, 2 * CHUNK], BF16, name=f"late{c}", align_bytes=256) for c in range(CHUNKS)}
+        y_ends = [keep.tile([P, CHUNK], F32, name=f"y_end{i}", align_bytes=256) for i in range(2)]
         y = [y_ends[0][:], late[2][:].bitcast(F32), late[3][:].bitcast(F32), y_ends[1][:]]
         bias_rest = keep.tile([P, E // 2], F32, name="bias_rest")
         bias_parked = [late[c][:, CHUNK + C - 2 : CHUNK + C + 2].bitcast(F32) for c in HELD]
         bias = [half[:, e : e + 1] for half in bias_parked for e in range(PER_CHUNK)]
         bias.extend(bias_rest[:, e : e + 1] for e in range(E // 2))
         gates = [keep.tile([P, CHUNK], F32, name=f"gate{c}", align_bytes=256) for c in range(CHUNKS)]
-        residual = keep.tile([P, T], F32, name="residual", align_bytes=256)
+        residual = keep.tile([P, T], F32, name="residual", align_bytes=4096)
         window = keep.tile([P, T], F32, name="window", align_bytes=256)
-        identity = keep.tile([P, P], F32, name="identity")
+        identity = keep.tile([P, P], F32, name="identity", align_bytes=256)
 
         nc.vector.memset(w_bytes[:].bitcast(I32), 0)
         x_rows = xT.rearrange("(p t) w -> p t w", t=PACK)
@@ -78,8 +78,8 @@ def tile_moe_res_lin_silu_kernel(tc, xT, xr, w_words, w_scales, b, gate, offs, o
         nc.sync.dma_start(residual[:], xr)
 
         ones = keep.tile([P, P], F32, name="ones")
-        column = keep.tile([P, P], F32, name="column", align_bytes=64)
-        turned_column = keep.tile([P, P], F32, name="turned_column", align_bytes=64)
+        column = keep.tile([P, P], F32, name="column", align_bytes=256)
+        turned_column = keep.tile([P, P], F32, name="turned_column", align_bytes=256)
         nc.vector.memset(ones[:], 1.0)
         nc.vector.tensor_tensor_scan(column[:], ones[:], ones[:], -1.0, MULT, ADD)
         nc.vector.transpose(turned_column[:], column[:])
@@ -113,8 +113,8 @@ def tile_moe_res_lin_silu_kernel(tc, xT, xr, w_words, w_scales, b, gate, offs, o
             rows = early[c] if t < 2 else late[c]
             copy(slots(c)[:, first:stop, t : t + 2], rows[:].rearrange("p (t n) -> p n t", t=2)[:, first:stop, :])
 
-        codes = [keep.tile([P, CHUNK], U32, name=f"codes{c}", align_bytes=64) for c in range(CHUNKS)]
-        scales = [keep.tile([P, CHUNK], U8, name=f"scales{c}", align_bytes=64) for c in range(CHUNKS)]
+        codes = [keep.tile([P, CHUNK], U32, name=f"codes{c}", align_bytes=256) for c in range(CHUNKS)]
+        scales = [keep.tile([P, CHUNK], U8, name=f"scales{c}", align_bytes=256) for c in range(CHUNKS)]
 
         def quantise(c, edges):
             for first, stop in zip(edges, edges[1:]):
@@ -201,11 +201,11 @@ def tile_moe_res_lin_silu_kernel(tc, xT, xr, w_words, w_scales, b, gate, offs, o
             turn_onto(u, residual, True)
         scatter(CHUNKS - 1)
 
-        turned = [keep.tile([P, UNIT], F32, name=f"turned{u}") for u in range(UNITS)]
+        turned = [keep.tile([P, UNIT], F32, name=f"turned{u}", align_bytes=256) for u in range(UNITS)]
         for u in range(UNITS):
             turn_onto(u, window, False)
             nc.scalar.copy(turned[u][:], sums[u][:])
-        last = keep.tile([P, T - shared], F32, name="last", align_bytes=256)
+        last = keep.tile([P, T - shared], F32, name="last", align_bytes=4096)
         for u in range(UNITS):
             back = psum.tile([P, UNIT], F32, name="back", tag="bank", bufs=BANKS)
             for h in range(2):
@@ -215,7 +215,7 @@ def tile_moe_res_lin_silu_kernel(tc, xT, xr, w_words, w_scales, b, gate, offs, o
 
         first = 0
         for i, width in enumerate(ADD_WIDTHS):
-            res = keep.tile([P, width], F32, name=f"res{i}", align_bytes=256)
+            res = keep.tile([P, width], F32, name=f"res{i}", align_bytes=512)
             nc.vector.tensor_tensor(res[:], window[:, first : first + width], residual[:, first : first + width], ADD)
             nc.sync.dma_start(out[:, first : first + width], res[:])
             first += width

@@ -41,7 +41,7 @@ def tile_moe_res_lin_silu_kernel(tc, xT, xr, w_words, w_scales, b, gate, offs, o
 
         offsets = keep.tile([P, SLOTS // 16], U16, name="offsets", align_bytes=256)
         planes = [keep.tile([P, T], F32, name=f"plane{t}", align_bytes=4096) for t in range(PACK)]
-        w_codes = [keep.tile([P, PER_CHUNK, N], U32, name=f"w_codes{c}", align_bytes=256) for c in range(CHUNKS)]
+        w_codes = [keep.tile([P, E // 2, N], U32, name=f"w_codes{h}", align_bytes=256) for h in range(2)]
         w_bytes = keep.tile([P, E, N], U8, name="w_bytes", align_bytes=256)
         grouped = [keep.tile([P, PACK * CHUNK], BF16, name=f"grouped{c}", align_bytes=256) for c in range(CHUNKS)]
         early = {c: keep.tile([P, 2 * CHUNK], BF16, name=f"early{c}", align_bytes=256) for c in HELD}
@@ -52,7 +52,7 @@ def tile_moe_res_lin_silu_kernel(tc, xT, xr, w_words, w_scales, b, gate, offs, o
         bias_parked = [late[c][:, CHUNK + C - 2 : CHUNK + C + 2].bitcast(F32) for c in HELD]
         bias = [half[:, e : e + 1] for half in bias_parked for e in range(PER_CHUNK)]
         bias.extend(bias_rest[:, e : e + 1] for e in range(E // 2))
-        gates = [keep.tile([P, CHUNK], F32, name=f"gate{c}", align_bytes=256) for c in range(CHUNKS)]
+        gates = [keep.tile([P, 2 * CHUNK], F32, name=f"gate{h}", align_bytes=256) for h in range(2)]
         residual = keep.tile([P, T], F32, name="residual", align_bytes=4096)
         window = keep.tile([P, T], F32, name="window", align_bytes=256)
         identity = keep.tile([P, P], F32, name="identity", align_bytes=256)
@@ -67,14 +67,13 @@ def tile_moe_res_lin_silu_kernel(tc, xT, xr, w_words, w_scales, b, gate, offs, o
         for q in range(4):
             nc.sync.dma_start(w_bytes[32 * q : 32 * q + 4, :, :].bitcast(I32), s_rows[4 * q : 4 * q + 4, :, :].bitcast(I32))
         w_rows = w_words.rearrange("e a p n r -> p (e a) (n r)").bitcast(I32)
-        for c in range(CHUNKS):
-            experts = slice(c * PER_CHUNK, (c + 1) * PER_CHUNK)
-            nc.sync.dma_start(w_codes[c][:].bitcast(I32), w_rows[:, experts, :])
-            if c < len(bias_parked):
-                nc.sync.dma_start(bias_parked[c], b[:, experts])
-            if c == len(bias_parked):
-                nc.sync.dma_start(bias_rest[:], b[:, E // 2 :])
-            nc.sync.dma_start(gates[c][:], gate[:, c * CHUNK : (c + 1) * CHUNK])
+        nc.sync.dma_start(w_codes[0][:].bitcast(I32), w_rows[:, : E // 2, :])
+        nc.sync.dma_start(bias_parked[0], b[:, :PER_CHUNK])
+        nc.sync.dma_start(gates[0][:], gate[:, : 2 * CHUNK])
+        nc.sync.dma_start(bias_parked[1], b[:, PER_CHUNK : E // 2])
+        nc.sync.dma_start(w_codes[1][:].bitcast(I32), w_rows[:, E // 2 :, :])
+        nc.sync.dma_start(bias_rest[:], b[:, E // 2 :])
+        nc.sync.dma_start(gates[1][:], gate[:, 2 * CHUNK :])
         nc.sync.dma_start(residual[:], xr)
 
         ones = keep.tile([P, P], F32, name="ones")
@@ -131,7 +130,7 @@ def tile_moe_res_lin_silu_kernel(tc, xT, xr, w_words, w_scales, b, gate, offs, o
                 bank = psum.tile([P, stop - first], F32, name="bank", tag="bank", bufs=BANKS)
                 nc.tensor.matmul_mx(
                     out=bank[:],
-                    lhsT=w_codes[c][:, e % PER_CHUNK, :].bitcast(FP8X4),
+                    lhsT=w_codes[c // 2][:, e % (E // 2), :].bitcast(FP8X4),
                     lhsT_scale=w_bytes[:, e, :],
                     rhs=codes[c][:, cols].bitcast(FP8X4),
                     rhs_scale=scales[c][:, cols],
@@ -141,7 +140,7 @@ def tile_moe_res_lin_silu_kernel(tc, xT, xr, w_words, w_scales, b, gate, offs, o
                 nc.scalar.activation(y[c][:, cols], bank[:], SILU, bias=bias[e])
 
         def scatter(c):
-            nc.vector.tensor_tensor(window[:].indirect(listed(c)), y[c], gates[c][:], MULT)
+            nc.vector.tensor_tensor(window[:].indirect(listed(c)), y[c], gates[c // 2][:, (c % 2) * CHUNK : (c % 2 + 1) * CHUNK], MULT)
 
         on_vector, on_scalar = nc.vector.tensor_copy, nc.scalar.copy
         halves = (0, C, CHUNK)

from contextlib import ExitStack

import concourse.mybir as mybir

K, T, E, C, N = 512, 4096, 8, 256, 128
SLOTS = E * C
FLOPS = 2 * SLOTS * K * N

F32 = mybir.dt.float32
BF16 = mybir.dt.bfloat16
U32 = mybir.dt.uint32
I32 = mybir.dt.int32
U16 = mybir.dt.uint16
U8 = mybir.dt.uint8
FP8X4 = mybir.dt.float8_e4m3fn_x4
MULT = mybir.AluOpType.mult
ADD = mybir.AluOpType.add
EQUAL = mybir.AluOpType.is_equal
COPY = mybir.ActivationFunctionType.Copy
SILU = mybir.ActivationFunctionType.Silu

P = 128
PACK = 4
CHUNK = 2 * C
CHUNKS = SLOTS // CHUNK
PER_CHUNK = CHUNK // C
PART = C // 2
HELD = (2, 3)
ADD_WIDTHS = (256, 384, 512, 512, 640, 768)
UNIT = 2 * P
UNITS = (T - sum(ADD_WIDTHS)) // UNIT
TABLE_COLUMNS = 8
BANKS = 4


def tile_moe_res_lin_silu_kernel(tc, xT, xr, w_words, w_scales, b, gate, offs, out):
    nc = tc.nc
    with ExitStack() as ctx:
        keep = ctx.enter_context(tc.tile_pool(name="keep", bufs=1))
        psum = ctx.enter_context(tc.psum_pool(name="psum", bufs=1))

        offsets = keep.tile([P, SLOTS // 16], U16, name="offsets", align_bytes=256)
        planes = [keep.tile([P, T], F32, name=f"plane{t}", align_bytes=4096) for t in range(PACK)]
        w_codes = [keep.tile([P, E // 2, N], U32, name=f"w_codes{h}", align_bytes=256) for h in range(2)]
        w_bytes = keep.tile([P, E, N], U8, name="w_bytes", align_bytes=256)
        grouped = [keep.tile([P, PACK * CHUNK], BF16, name=f"grouped{c}", align_bytes=256) for c in range(CHUNKS)]
        early = {c: keep.tile([P, 2 * CHUNK], BF16, name=f"early{c}", align_bytes=256) for c in HELD}
        late = {c: keep.tile([P, 2 * CHUNK], BF16, name=f"late{c}", align_bytes=256) for c in range(CHUNKS)}
        y_ends = [keep.tile([P, CHUNK], F32, name=f"y_end{i}", align_bytes=256) for i in range(2)]
        y = [y_ends[0][:], late[2][:].bitcast(F32), late[3][:].bitcast(F32), y_ends[1][:]]
        bias_rest = keep.tile([P, E // 2], F32, name="bias_rest")
        bias_parked = [late[c][:, CHUNK + C - 2 : CHUNK + C + 2].bitcast(F32) for c in HELD]
        bias = [half[:, e : e + 1] for half in bias_parked for e in range(PER_CHUNK)]
        bias.extend(bias_rest[:, e : e + 1] for e in range(E // 2))
        gates = [keep.tile([P, 2 * CHUNK], F32, name=f"gate{h}", align_bytes=256) for h in range(2)]
        residual = keep.tile([P, T], F32, name="residual", align_bytes=4096)
        window = keep.tile([P, T], F32, name="window", align_bytes=256)
        identity = keep.tile([P, P], F32, name="identity", align_bytes=256)

        nc.vector.memset(w_bytes[:].bitcast(I32), 0)
        x_rows = xT.rearrange("(p t) w -> p t w", t=PACK)
        nc.sync.dma_start(planes[0][:], x_rows[:, 0, :])
        nc.sync.dma_start(offsets[:], offs)
        for t in range(1, PACK):
            nc.sync.dma_start(planes[t][:], x_rows[:, t, :])
        s_rows = w_scales.rearrange("e a q n -> q (e a) n")
        for q in range(4):
            nc.sync.dma_start(w_bytes[32 * q : 32 * q + 4, :, :].bitcast(I32), s_rows[4 * q : 4 * q + 4, :, :].bitcast(I32))
        w_rows = w_words.rearrange("e a p n r -> p (e a) (n r)").bitcast(I32)
        nc.sync.dma_start(w_codes[0][:].bitcast(I32), w_rows[:, : E // 2, :])
        nc.sync.dma_start(bias_parked[0], b[:, :PER_CHUNK])
        nc.sync.dma_start(gates[0][:], gate[:, : 2 * CHUNK])
        nc.sync.dma_start(bias_parked[1], b[:, PER_CHUNK : E // 2])
        nc.sync.dma_start(w_codes[1][:].bitcast(I32), w_rows[:, E // 2 :, :])
        nc.sync.dma_start(bias_rest[:], b[:, E // 2 :])
        nc.sync.dma_start(gates[1][:], gate[:, 2 * CHUNK :])
        nc.sync.dma_start(residual[:], xr)

        ones = keep.tile([P, P], F32, name="ones")
        column = keep.tile([P, P], F32, name="column", align_bytes=256)
        turned_column = keep.tile([P, P], F32, name="turned_column", align_bytes=256)
        nc.vector.memset(ones[:], 1.0)
        nc.vector.tensor_tensor_scan(column[:], ones[:], ones[:], -1.0, MULT, ADD)
        nc.vector.transpose(turned_column[:], column[:])
        for q in range(0, P, 32):
            nc.vector.tensor_scalar(identity[q : q + 32, :], column[q : q + 32, :], turned_column[q : q + 32, q : q + 1], None, EQUAL)

        nc.vector.memset(window[:, :TABLE_COLUMNS], 0.0)
        nc.vector.memset(window[:, TABLE_COLUMNS:], 0.0)
        nc.scalar.activation(window[:, :TABLE_COLUMNS], window[:, :TABLE_COLUMNS], SILU)

        def listed(c, first=0, stop=CHUNK):
            return offsets[:, (c * CHUNK + first) // 16 : (c * CHUNK + stop) // 16]

        def slots(c):
            return grouped[c][:].rearrange("p (n t) -> p n t", t=PACK)

        def gather_placed(t, c):
            nc.vector.tensor_copy(slots(c)[:, :, t], planes[t][:].indirect(listed(c)))

        def row(t, c, first, stop):
            rows = early[c] if t < 2 else late[c]
            return rows[:, (t % 2) * CHUNK + first : (t % 2) * CHUNK + stop]

        def gather_vector(t, c, first=0, stop=CHUNK):
            nc.vector.tensor_copy(row(t, c, first, stop), planes[t][:].indirect(listed(c, first, stop)))

        def gather_scalar(t, c, first=0, stop=CHUNK):
            nc.scalar.activation(row(t, c, first, stop), planes[t][:].indirect(listed(c, first, stop)), COPY)

        def weave(copy, t, c, first=0, stop=CHUNK):
            rows = early[c] if t < 2 else late[c]
            copy(slots(c)[:, first:stop, t : t + 2], rows[:].rearrange("p (t n) -> p n t", t=2)[:, first:stop, :])

        codes = [keep.tile([P, CHUNK], U32, name=f"codes{c}", align_bytes=256) for c in range(CHUNKS)]
        scales = [keep.tile([P, CHUNK], U8, name=f"scales{c}", align_bytes=256) for c in range(CHUNKS)]

        def quantise(c, edges):
            for first, stop in zip(edges, edges[1:]):
                nc.vector.quantize_mx(
                    out=codes[c][:, first:stop].bitcast(FP8X4),
                    scales=scales[c][:, first:stop],
                    in_=grouped[c][:, PACK * first : PACK * stop],
                )

        def multiply(c, edges):
            for first, stop in zip(edges, edges[1:]):
                e = (c * CHUNK + first) // C
                cols = slice(first, stop)
                bank = psum.tile([P, stop - first], F32, name="bank", tag="bank", bufs=BANKS)
                nc.tensor.matmul_mx(
                    out=bank[:],
                    lhsT=w_codes[c // 2][:, e % (E // 2), :].bitcast(FP8X4),
                    lhsT_scale=w_bytes[:, e, :],
                    rhs=codes[c][:, cols].bitcast(FP8X4),
                    rhs_scale=scales[c][:, cols],
                    start=True,
                    stop=True,
                )
                nc.scalar.activation(y[c][:, cols], bank[:], SILU, bias=bias[e])

        def scatter(c):
            nc.vector.tensor_tensor(window[:].indirect(listed(c)), y[c], gates[c // 2][:, (c % 2) * CHUNK : (c % 2 + 1) * CHUNK], MULT)

        on_vector, on_scalar = nc.vector.tensor_copy, nc.scalar.copy
        halves = (0, C, CHUNK)

        for t in range(2):
            gather_placed(t, 0)
            gather_placed(t, 1)
            gather_scalar(t, 3)
            gather_scalar(t, 2)
        weave(on_vector, 0, 3)
        weave(on_scalar, 0, 2)
        gather_vector(2, 0)
        gather_vector(2, 3)
        gather_scalar(2, 1)
        gather_scalar(2, 2)

        gather_vector(3, 0, 0, PART)
        gather_vector(3, 0, PART, C)
        gather_scalar(3, 0, C, CHUNK)
        for first in (0, C):
            gather_scalar(3, 1, first, first + C)
        weave(on_scalar, 2, 1, 0, PART)
        last_part = CHUNK - PART
        for first in range(0, last_part, PART):
            weave(on_vector, 2, 0, first, first + PART)
        quantise(0, (0, PART))
        weave(on_vector, 2, 0, last_part, CHUNK)
        quantise(0, range(PART, CHUNK + 1, PART))
        weave(on_vector, 2, 1, PART, C)
        weave(on_vector, 2, 1, C, CHUNK)
        quantise(1, halves)
        multiply(0, range(0, CHUNK + 1, PART))
        scatter(0)

        for c in HELD:
            for first in (0, C):
                gather_scalar(3, c, first, first + C)
            for first in (0, C):
                weave(on_scalar, 2, c, first, first + C)
            quantise(c, (0, CHUNK))
            multiply(c - 1, halves)
            scatter(c - 1)
        multiply(CHUNKS - 1, halves)

        shared = sum(ADD_WIDTHS)
        sums = [psum.tile([P, UNIT], F32, name=f"sum{u}") for u in range(UNITS)]

        def turn_onto(u, source, opens):
            for h in range(2):
                first = shared + u * UNIT + h * P
                nc.tensor.matmul(
                    sums[u][:, h * P : (h + 1) * P], source[:, first : first + P], identity[:],
                    start=opens and h == 0, stop=not opens and h == 1, is_transpose=True,
                )

        for u in range(UNITS):
            turn_onto(u, residual, True)
        scatter(CHUNKS - 1)

        turned = [keep.tile([P, UNIT], F32, name=f"turned{u}", align_bytes=256) for u in range(UNITS)]
        for u in range(UNITS):
            turn_onto(u, window, False)
            nc.scalar.copy(turned[u][:], sums[u][:])
        last = keep.tile([P, T - shared], F32, name="last", align_bytes=4096)
        for u in range(UNITS):
            back = psum.tile([P, UNIT], F32, name="back", tag="bank", bufs=BANKS)
            for h in range(2):
                nc.tensor.transpose(back[:, h * P : (h + 1) * P], turned[u][:, h * P : (h + 1) * P], identity[:])
            at = u * UNIT
            nc.scalar.copy(last[:, at : at + UNIT], back[:])

        first = 0
        for i, width in enumerate(ADD_WIDTHS):
            res = keep.tile([P, width], F32, name=f"res{i}", align_bytes=512)
            nc.vector.tensor_tensor(res[:], window[:, first : first + width], residual[:, first : first + width], ADD)
            nc.sync.dma_start(out[:, first : first + width], res[:])
            first += width
        nc.sync.dma_start(out[:, shared:], last[:])
